import numpy as np, ml_dtypes
CORES = [13,21,141,149]
N = 4
BF = ml_dtypes.bfloat16
def gentries(a):
    return np.ascontiguousarray(a.reshape(8, 16, -1).transpose(0, 2, 1)).reshape(8, -1)
def gtable(e):
    e = np.asarray(e); return np.ascontiguousarray(e.reshape(8, -1, 16).transpose(0, 2, 1)).reshape(128, -1).astype(np.int32)
D, B, W, K, NB, S, RO = 4, 3, 4096, 2048, 128, 32, 3
def parts(rng):
    return rng.integers(0, 256, (N, 8, 16, W)), rng.integers(0, W, (N, 8, K)), rng.integers(0, 256, (N, 8, 16, NB)), rng.integers(900, 1701, (N, 8, RO))
def pack(X, L, z, t):
    return {"x0": np.ascontiguousarray(X.reshape(N, 128, W)).astype(np.float32).astype(BF), "l0": np.stack([gtable(a) for a in L]),
            "z0": np.ascontiguousarray(z.reshape(N, 128, NB)).astype(np.float32).astype(BF), "th": np.ascontiguousarray(t).astype(np.int32)}
def setup_inputs(rng):
    return pack(*parts(rng))
def setup_inputs_spread(rng):
    X = np.minimum((np.exp2(8 * rng.random((N, 8, 1, W))) * rng.random((N, 8, 16, W))).astype(np.int64), 255)
    z = np.minimum((np.exp2(8 * rng.random((N, 8, 1, NB))) * rng.random((N, 8, 16, NB))).astype(np.int64), 255)
    L = np.minimum((W * rng.random((N, 8, K)) ** rng.choice(np.array([1.0, 2.0, 4.0]), (N, 8, 1))).astype(np.int64), W - 1)
    t = np.minimum(np.exp2(12 * rng.random((N, 8, RO))).astype(np.int64), 4080)
    return pack(X, L, z, t)
def setup_inputs_ends(rng):
    X = 255 * rng.integers(0, 2, (N, 8, 16, W)); X = np.where(rng.random((N, 8, 1, W)) < 0.5, 255 * rng.integers(0, 2, (N, 8, 1, W)), X)
    z = 255 * rng.integers(0, 2, (N, 8, 16, NB)); z = np.where(rng.random((N, 8, 1, NB)) < 0.5, 255 * rng.integers(0, 2, (N, 8, 1, NB)), z)
    sw = rng.integers(0, 2, (N, 8, 1)); X[..., 0] = 255 * sw; X[..., W - 1] = 255 * (1 - sw)
    z[..., 0] = 255 * rng.integers(0, 2, (N, 8, 1)); z[..., NB - 1] = 255 * rng.integers(0, 2, (N, 8, 1))
    L = (W - 1) * rng.integers(0, 2, (N, 8, K)); m = rng.random((N, 8, K)) < 0.25; m[:, 1::2] = False
    L = np.where(m, rng.integers(0, W, (N, 8, K)), L)
    L[..., 0] = W - 1; L[..., 1] = 0; L[..., K - 2] = 0; L[..., K - 1] = W - 1
    t = 4080 * rng.integers(0, 2, (N, 8, RO)); t[:, 0, 0] = 0; t[:, 1, 0] = 4080
    L[:, 5] = 0; L[:, 6] = W - 1; L[:, 7] = 0; X[:, 7] = 0; X[:, 7, :, 0] = 255; X[:, 7, :, W - 1] = 255; z[:, 7] = 0; t[:, 7, 0] = 0
    b = int(rng.integers(0, 2))
    for r in range(N):
        if (r + b) & 1: L[r, 7, K - 1] = 1
    return pack(X, L, z, t)
def setup_inputs_corners(rng):
    X, L, z, t = parts(rng); t = rng.integers(100, 3600, (N, 8, RO)); t[:, :, 0] = rng.integers(300, 2000, (N, 8))
    z = np.where(rng.random((N, 8, 1, NB)) < 0.5, 255 * rng.integers(0, 2, (N, 8, 1, NB)), z)
    for r in range(N):
        kinds = rng.permutation(8)
        for g in range(8):
            j = int(kinds[g]); beg = np.zeros(K, np.int64)
            if j == 0: t[r, g, 0] = rng.choice(np.array([300, 4080]))
            elif j == 1: beg[:] = 1; t[r, g, 0] = rng.choice(np.array([0, 3000]))
            elif j == 2: beg[K - 1] = 1
            elif j == 3: beg[1] = 1
            elif j == 4: beg[::2] = 1
            elif j == 5: beg[::3] = 1
            elif j == 6:
                c = np.add.accumulate(rng.choice(np.array([1, 2, 3, 4, 5, 15, 16, 17, 64, 255, 256, 257]), K)); beg[c[c < K]] = 1
            else: beg[K // 2 + 1] = 1
            beg[0] = 1; cl = np.add.accumulate(beg) & 1
            bit = rng.integers(0, 2, W); bit[0] = 0; bit[W - 1] = 1
            X[r, g] = rng.integers(0, 16, (16, W)) + 240 * bit
            a0 = np.flatnonzero(bit == 0); a1 = np.flatnonzero(bit == 1)
            n = np.where(cl == 1, a1[rng.integers(0, len(a1), K)], a0[rng.integers(0, len(a0), K)])
            L[r, g] = np.where(rng.random(K) < 0.2, (W - 1) * cl, n)
    return pack(X, L, z, t)
def late(rng, X, L, z, t, dg):
    k = np.arange(K); c = np.arange(W); h = B * (D - 1)
    n = 32 * int(rng.integers(0, 9)) + int(rng.integers(8, 25)); R = np.zeros(K, np.int64); R[rng.permutation(K)[:n]] = 1
    for g in range(8):
        r = (g - dg) % N
        a = 8 * rng.integers(0, 17, (8, 1)); e = 8 * rng.integers(4, 11, (8, 1)); v = 8 * rng.integers(4, 26, (7, 1)); q = int(np.sum(e))
        X[r, g] = np.concatenate([a + e * (((c >> h) & 1) ^ rng.integers(0, 2, (8, 1))), v * ((c >> (h + 1)) & 1), np.full((1, W), 4)])
        z[r, g, 8:15] = v * (g & 1)
        m = rng.integers(0, W, K)
        for j in range(D): m = (m & ~(1 << (B * j))) | ((k & 1) << (B * j))
        m = m & ~4
        L[r, g] = (m & ~(2 << h)) | (((g & 1) ^ R) << (h + 1))
        t[r, g, 0] = rng.integers(0, q); t[r, g, 1] = q - 1 - (n & 31); t[r, g, 2:] = q - rng.integers(1, 9, RO - 2)
def few(rng, X, L, z, t, dg):
    k = np.arange(K); c = np.arange(W); h = B * (D - 1); o = int(rng.integers(0, 8))
    rows = 16 * rng.permutation(NB)[:3] + rng.integers(0, 16, 3)
    b = np.zeros((8, 3), np.int64)
    for j, st in enumerate(((0, 3), (0, 3), (0, 5))):
        for s in st: b[(s + o) % 8, j] = 1; b[(s + 1 + o) % 8, j] = 1
    zb = b * (RO & 1); w = b; u = zb; n = np.zeros((8, RO), np.int64)
    for rnd in range(1, RO):
        take = (w != u) & (np.roll(w, 1, axis=0) == u); w = np.where(take, u, w); u = np.abs(w - u); n[:, rnd] = np.add.reduce(take.astype(np.int64), axis=1)
    for g in range(8):
        r = (g - dg) % N
        a = 8 * rng.integers(0, 2, (11, 1)); e = 8 * rng.integers(24, 31, (11, 1)); v = 8 * rng.integers(4, 26, (4, 1)); q = int(np.sum(e))
        X[r, g] = np.concatenate([a + e * (((c >> h) & 1) ^ rng.integers(0, 2, (11, 1))), v * ((c >> (h + 1)) & 1), np.full((1, W), 4)])
        zz = z[r, g]; zz[11:15, rows >> 4] = v * zb[g]
        bt = np.zeros(K, np.int64); bt[rows] = b[g]
        L[r, g] = (rng.integers(0, W, K) & ~(3 << h) & ~4) | ((k & 1) << h) | (bt << (h + 1))
        t[r, g, 0] = rng.integers(0, q); t[r, g, 1:] = q - 1 - n[g, 1:]; t[r, g, RO - 1] = q - max(int(n[g, RO - 1]), 1)
def setup_inputs_crowd(rng):
    X = rng.integers(0, 8, (N, 8, 16, W)); z = rng.integers(0, 8, (N, 8, 16, NB)); L = np.zeros((N, 8, K), np.int64)
    t = rng.choice(np.array([0, 10, 20]), (N, 8, RO)); t[:, :, 0] = 0; rep = (W - 1) // (2 ** B - 1)
    dg = int(rng.integers(0, N))
    for r in range(N):
        kinds = rng.permutation(np.array([0, 1, 2, 3, 4, 0, 1, 4])[:8 - 8 // N]); i = 0
        for g in range(8):
            if (g - r) % N == dg: continue
            p = g & 1; ds = np.arange(p + 2, 2 ** B, 2); xv = X[r, g]; kind = int(kinds[i]); i += 1
            xv[:, ds * rep] = rng.integers(128, 256, (16, len(ds))); xv[0, ds * rep] = 128 + ds
            if kind == 4:
                e = ds[rng.integers(0, len(ds), NB)] * rep; L[r, g] = np.repeat(e, 16); z[r, g] = xv[:, e]
            else:
                d = ds[rng.integers(0, len(ds), K)] * rep
                if kind > 0:
                    k0 = (K - 1, 0, int(rng.integers(1, K - 1)))[kind - 1]; d[k0] = p * rep; z[r, g, :, k0 // 16] = xv[:, p * rep]
                L[r, g] = d
    late(rng, X, L, z, t, dg)
    return pack(X, L, z, t)
def setup_inputs_ties(rng):
    X, L, z, t = parts(rng); odd = int(rng.integers(0, 2)); dg = int(rng.integers(0, N))
    for r in range(N):
        ring = np.flatnonzero((np.arange(8) - r) % N == dg); rest = rng.permutation(np.setdiff1d(np.arange(8), ring))
        p = np.concatenate([rest[:-1], ring, rest[-1:]]); tv = rng.permutation(np.array([0, 31, 4079, int(rng.integers(32, 4079))]))
        for i in range(4):
            g = int(p[i]); T = int(tv[i]); a = T // 16 + (np.arange(16) < T % 16); b = a + (np.arange(16) == T % 16)
            v = np.stack([np.zeros(16, np.int64), a, b])[:, rng.permutation(16)]
            X[r, g] = v[rng.integers(0, 3, W)].T
            t[r, g, 0] = T; t[r, g, 1:] = np.maximum(T - rng.integers(0, 32, RO - 1), 0)
        for i in range(4, 8):
            g = int(p[i]); c = np.arange(W); t[r, g] = rng.integers(700, 1300, RO)
            if i == 7:
                up = (r + odd) & 1; X[r, g] = 255 * up; z[r, g] = 255 * (1 - up)
                X[r, g, rng.integers(0, 16, W), c] += (1 - 2 * up) * rng.integers(0, 2, W)
                continue
            base = rng.integers(0, 201, 16)
            X[r, g] = base[(np.arange(16)[:, None] + rng.integers(0, 16, W)[None, :]) % 16]
            X[r, g, rng.integers(0, 16, W), c] += rng.integers(0, 2, W)
            z[r, g] = 255 * rng.integers(0, 2, (1, NB))
    few(rng, X, L, z, t, dg)
    return pack(X, L, z, t)
def check_inputs(d):
    bad = []
    for k, lo, hi in (("x0", 0, 255), ("l0", 0, W - 1), ("z0", 0, 255), ("th", 0, 4080)):
        v = np.asarray(d[k]).astype(np.float64)
        if not (np.min(v) >= lo and np.max(v) <= hi): bad.append("range of " + k)
        elif not np.all(v == np.floor(v)): bad.append("whole numbers in " + k)
    return bad
def reference(x0, l0, z0, th):
    X = x0.astype(np.float32).astype(np.int32).reshape(N, 8, 16, W); z = z0.astype(np.float32).astype(np.int32).reshape(N, 8, 16, NB)
    L = np.stack([gentries(a) for a in l0]).astype(np.int64); t = th.astype(np.int64); k = np.arange(K)
    x = np.take_along_axis(X, L[:, :, None, :], 3); A = np.zeros((N, 8), np.int64); low = 2 ** B - 1
    for rnd in range(RO):
        beg = np.ones((N, 8, K), bool)
        beg[..., 1:] = np.add.reduce(np.abs(x[..., 1:] - x[..., :-1]), axis=2) > (t[:, :, rnd] + (A & 31))[..., None]
        beg[..., 0] = True
        s = np.maximum.accumulate(np.where(beg, k, 0), axis=2)
        nx = np.minimum.accumulate(np.where(beg, k, K)[..., ::-1], axis=2)[..., ::-1]
        ln = np.concatenate([nx[..., 1:], np.full((N, 8, 1), K)], axis=2) - s
        P = np.zeros((N, 8, K), np.int64)
        for c in range(D):
            q = D * (k - s) + c; pl = np.zeros((N, 8, K), np.int64)
            for j in range(1, D): pl = pl + (q >= j * ln)
            P = (P << B) | ((np.take_along_axis(L, s + q - pl * ln, 2) >> (B * (D - 1 - pl))) & low)
        hi = np.roll(P >> (B * (D - 1)), (1, 1), axis=(0, 1)); lo = np.roll(P & low, (2, 2), axis=(0, 1))
        M = (hi << (B * (D - 1))) | (((P >> B) & (2 ** (B * (D - 2)) - 1)) << B) | lo
        y = np.take_along_axis(X, P[:, :, None, :], 3); y2 = np.take_along_axis(X, M[:, :, None, :], 3); zr = np.repeat(z, 16, axis=3)
        took = np.add.reduce(np.abs(y2 - zr), axis=2) < np.add.reduce(np.abs(y - zr), axis=2)
        L = np.where(took, M, P); x = np.where(took[:, :, None, :], y2, y); A = np.add.reduce(took.astype(np.int64), axis=2)
        Y = np.max(x.reshape(N, 8, 16, NB, 16), axis=4)
        if rnd < RO - 1:
            col = S * np.arange(NB) + (np.add.reduce(Y, axis=2) & (S - 1))
            np.put_along_axis(X, col[:, :, None, :].astype(np.int64), (Y + z) >> 1, 3)
        z = np.abs(Y - z)
    return {"ly": np.stack([gtable(a) for a in L]).astype(np.float32), "xy": x.reshape(N, 128, K).astype(np.float32).astype(BF), "zy": z.reshape(N, 128, NB).astype(np.float32).astype(BF)}

@@ -1,0 +1,509 @@
+from concourse.mybir import AluOpType as A, ActivationFunctionType as F
+
+RO = 3
+PITCH = 512
+S0 = 19 * PITCH
+TABW = S0 + 2048
+BIG = 4096.0
+MAG = 1536.0
+HC = MAG - 7.5 / 16
+
+bf, f16, f32, i32, u16 = "bfloat16", "float16", "float32", "int32", "uint16"
+SB = {
+    "X": (4096, bf), "tab": (TABW, bf), "xb": (2064, bf), "yy": (4096, bf), "aby": (2048, bf), "ab2": (2048, bf),
+    "G0": (2048, bf), "G1": (2048, bf), "ysc": (2048, bf), "E": (2048, bf), "zr": (2048, bf), "zsp": (2048, bf), "m16": (512, bf),
+    "li": (128, i32), "dgi": (512, i32), "src": (528, bf), "thi": (4, i32), "thf": (4, f32),
+    "za": (128, bf), "zb": (128, bf), "nzT": (128, bf), "zh": (128, i32),
+    "ox": (128, u16), "o0": (128, u16), "o1": (128, u16), "oP": (128, u16), "oM": (128, u16), "oc": (8, u16),
+    "ui": (8, i32), "um": (8, i32), "uf": (8, f32), "c32": (8, i32),
+    "ai": (4, i32), "am": (4, i32), "af": (4, f32), "thE": (384, f32), "aE": (128, bf), "Egf": (128, f32), "onf": (128, f32),
+    "vb": (128, bf), "stg": (128, f32), "st2": (128, f32), "st3": (128, f32), "gi": (8, i32), "gj": (8, i32),
+    "Ib": (128, bf), "nIb": (128, bf), "grp": (8, bf), "ngrp": (8, bf), "S": (144, bf), "s9": (16, bf), "s24": (24, bf),
+    "zer": (144, bf), "onF": (128, bf), "onB": (128, bf), "c16": (128, bf),
+    "kc": (128, f16), "dlt": (128, f16), "EF": (128, f16), "EB": (128, f16), "onh": (8, f16),
+    "nb": (144, bf), "il": (128, bf), "jl": (128, bf), "wl": (128, bf), "Ibuf": (144, f16), "Wbuf": (144, f16),
+    "ii": (128, f16), "jj": (128, f16), "cc": (384, f16), "cl": (384, f16), "h0": (128, f16), "h1": (128, f16),
+    "dv": (128, f16), "n3": (384, f16), "mm": (384, f16), "mb": (384, f16),
+    "ta": (384, f16), "tb": (384, f16), "took": (128, f16), "tk": (256, f16), "lo": (128, f32),
+}
+SCALES = [1, -1, 3, -3, 512, 1536, 128, -512, -8192, 2, 1024, 8, 64, 2048]
+for _s in SCALES:
+    SB["I%s%d" % ("m" if _s < 0 else "", abs(_s))] = (128, f16)
+for _t in range(RO):
+    SB["d0_%d" % _t] = (144, f16); SB["d3_%d" % _t] = (160, f16)
+    SB["hi_%d" % _t] = (128, f16); SB["lw_%d" % _t] = (128, f16); SB["rl_%d" % _t] = (128, f16)
+SCRATCH = {k: ("sbuf", [128, w], d) for k, (w, d) in SB.items()}
+for _b in range(8):
+    SCRATCH["P%d" % _b] = ("psum", [128, 512], f32)
+DSEMS = ["dl0", "dth", "dz", "dx0", "dx1", "oly", "ozy"] + ["oxy%d" % q for q in range(4)] \
+    + ["tm%d" % t for t in range(RO)] + ["ts%d" % t for t in range(RO)]
+SEMAPHORES = ["pe", "dve", "act", "pool", "sent"] + DSEMS \
+    + ["ah%d" % t for t in range(RO)] + ["al%d" % t for t in range(RO)] + ["ar%d" % t for t in range(RO)]
+
+F0, F1 = 3584, 7680
+GX, GY, GM = 512, 512, 256
+G0S, G1S = 1088, 1024
+EV = 1
+FUSE = 0
+
+
+def relay_of(src, dst, topo):
+    c = [k for k in topo.cores_of(src) if k != src and topo.may_write(k, dst)]
+    same = [k for k in c if topo.die(k) == topo.die(src)]
+    return (same or c)[0]
+
+
+def nbits(m):
+    return bin(m).count("1")
+
+
+def rank_program(g, core, T, topo):
+    cores = list(T.cores); N = len(cores)
+    rank = T.rank_of(core)
+    if rank is None:
+        for r in range(N):
+            src, dst = cores[r], cores[(r + 1) % N]
+            if not topo.may_write(src, dst) and relay_of(src, dst, topo) == core:
+                m_in = topo.mask(src, core) & topo.mask(src, cores[(r + 2) % N]); m = topo.mask(core, dst)
+                rid, pid = topo.addr(dst, core)
+                for t in range(RO):
+                    g.wait_ge(T.sem["ar%d" % t], nbits(m_in))
+                    g.remote_dma(T["hi_%d" % t][:], T["rl_%d" % t][:], T.sem["ah%d" % t], T.sem.sent, pid, rid, m)
+                g.wait_ge(T.sem.sent, RO * nbits(m))
+        return
+    Q = {"pe": g.tensor, "dve": g.vector, "act": g.scalar, "pool": g, "sp": g.sync}
+    cnt = {}; known = {q: {} for q in Q}; clock = {}; hist = {}
+
+    def psum(name): return name[0] == "P" and name[1:].isdigit()
+
+    def V(name, c0=None, c1=None, st=1, p0=0, p1=128):
+        if c0 is None: c0, c1 = 0, (512 if psum(name) else SB[name][0])
+        if st == 1: ap = T[name][p0:p1, c0:c1]
+        elif st > 0: ap = T[name][p0:p1, c0:c1:st]
+        else: ap = T[name][p0:p1, c1 - 1:(c0 - 1 if c0 > 0 else None):-1]
+        return (ap, name, c0, c1, abs(st), p0, p1)
+
+    def meet(a, e, pad):
+        if a[6] <= e[7] or e[8] <= a[5]: return False
+        a0, a1 = (a[2] // 8 * 8, (a[3] + 7) // 8 * 8) if pad else (a[2], a[3])
+        if not (e[0] < a1 and a0 < e[1]): return False
+        return pad or a[4] != e[6] or (a[2] - e[0]) % a[4] == 0
+
+    def wait(q, tok):
+        s, n = tok
+        if known[q].get(s, 0) >= n: return
+        Q[q].wait_ge(T.sem[s], n)
+        k = known[q]; k[s] = n
+        for s2, n2 in clock.get(tok, {}).items():
+            if k.get(s2, 0) < n2: k[s2] = n2
+
+    def emit(q, fn, R, W, sem=None, after=(), last=True, grp_tok=None):
+        dma = sem is not None
+        need = {}
+        acc_all = [(r, False) for r in R] + [(w, True) for w in W]
+        for acc, wr in acc_all:
+            ps = psum(acc[1])
+            for e in hist.get(acc[1], []):
+                w2, q2, tok, d2 = e[2:6]
+                if ps:
+                    if q2 == q and (q == "pe" or not ((wr or w2) and meet(acc, e, False))): continue
+                else:
+                    if not (wr or w2) or not meet(acc, e, wr and w2 and dma != d2): continue
+                    if dma and d2 and tok[0] == sem: continue
+                if need.get(tok[0], 0) < tok[1]: need[tok[0]] = tok[1]
+        for tok in after:
+            if need.get(tok[0], 0) < tok[1]: need[tok[0]] = tok[1]
+        for s, n in sorted(need.items(), key=lambda e: -len(clock.get(e, {}))): wait(q, (s, n))
+        ins = fn()
+        s = sem if dma else q
+        inc = 16 if dma else 1
+        if last:
+            ins.then_inc(T.sem[s], inc); cnt[s] = cnt.get(s, 0) + inc
+            tok = grp_tok or (s, cnt[s])
+        else:
+            tok = (s, cnt.get(s, 0) + 1)
+        c = clock.setdefault(tok, {})
+        for s2, n2 in known[q].items():
+            if c.get(s2, 0) < n2: c[s2] = n2
+        for acc, wr in acc_all:
+            h = hist.setdefault(acc[1], [])
+            if wr and acc[4] == 1:
+                h[:] = [e for e in h if not (acc[2] <= e[0] and e[1] <= acc[3] and acc[5] <= e[7] and e[8] <= acc[6]
+                                             and (e[4][0] == tok[0] or known[q].get(e[4][0], 0) >= e[4][1]))]
+            h.append((acc[2], acc[3], wr, q, tok, dma, acc[4], acc[5], acc[6]))
+        return tok
+
+    def sc(x): return x[0] if isinstance(x, tuple) else x
+
+    def mm(out, lhsT, rhs, start, stop, last=None, after=()):
+        return emit("pe", lambda: g.tensor.matmul(out[0], lhsT[0], rhs[0], start, stop), [lhsT, rhs], [out],
+                    last=stop if last is None else last, after=after)
+    def group(out, terms, start=True, stop=True, last=None):
+        for n, (l, r) in enumerate(terms):
+            e = n == len(terms) - 1
+            mm(out, l, r, start and n == 0, stop and e, last=(e and (stop if last is None else last)))
+    def ts(out, in0, s1, s2, op0, op1=None):
+        R = [in0] + [s for s in (s1, s2) if isinstance(s, tuple)]
+        if op1 is None:
+            return emit("dve", lambda: g.vector.tensor_scalar(out[0], in0[0], sc(s1), None, op0), R, [out])
+        return emit("dve", lambda: g.vector.tensor_scalar(out[0], in0[0], sc(s1), sc(s2), op0, op1), R, [out])
+    def tt(out, a, b, op):
+        return emit("dve", lambda: g.vector.tensor_tensor(out[0], a[0], b[0], op), [a, b], [out])
+    def cp(out, a):
+        return emit("dve", lambda: g.vector.tensor_copy(out[0], a[0]), [a], [out])
+    def ms(out, v):
+        return emit("dve", lambda: g.vector.memset(out[0], v), [], [out])
+    def scan(out, d0, d1, init, op0, op1):
+        return emit("dve", lambda: g.vector.tensor_tensor_scan(out[0], d0[0], d1[0], init, op0, op1), [d0, d1], [out])
+    def act(out, a, f, bias=0.0, scale=1.0):
+        return emit("act", lambda: g.scalar.activation(out[0], a[0], f, bias=bias, scale=scale), [a], [out])
+    def gat(q, name, c0, win, off, a, b):
+        out, o = V(name, c0 + a, c0 + b), V(off, a // 16, b // 16)
+        if q == "dve":
+            return emit(q, lambda: g.vector.tensor_copy(out[0], win[0].indirect(o[0])), [win, o], [out])
+        return emit(q, lambda: g.scalar.activation(out[0], win[0].indirect(o[0]), F.Copy), [win, o], [out])
+    def iota(out, pat, base, cm):
+        if SB[out[1]][1] == i32:
+            return emit("pool", lambda: g.iota(out[0], pat, base, cm), [], [out])
+        return emit("pool", lambda: g.iota(out[0], pat, base, cm, allow_small_or_imprecise_dtypes=True), [], [out])
+    def dma(q, sem, out, in_, R, W, grp_tok=None):
+        return emit(q, lambda: Q[q].dma_start(out, in_), R, W, sem=sem, grp_tok=grp_tok)
+    def I(s): return V("I%s%d" % ("m" if s < 0 else "", abs(s)))
+    def P(b, c0=0, c1=128, st=1, p0=0, p1=128): return V("P%d" % b, c0, c1, st, p0, p1)
+
+    nxt, nx2, prv = cores[(rank + 1) % N], cores[(rank + 2) % N], cores[(rank - 1) % N]
+    m2 = topo.mask(core, nx2)
+    direct = topo.may_write(core, nxt)
+    hop = nxt if direct else relay_of(core, nxt, topo)
+    m1 = topo.mask(core, hop) & m2
+    n_hi = nbits(topo.mask(prv, core) & topo.mask(prv, nxt)) if topo.may_write(prv, core) \
+        else nbits(topo.mask(relay_of(prv, core, topo), core))
+    n_lo = nbits(topo.mask(cores[(rank - 2) % N], core))
+    sent = [0]
+
+    def send(dst, name, buf, sem, mask):
+        rid, pid = topo.addr(dst, core)
+        for e in hist.get(buf[1], []):
+            if e[2]: wait("pool", e[4])
+        g.remote_dma(T[name][:], buf[0], T.sem[sem], T.sem.sent, pid, rid, mask)
+        sent[0] += nbits(mask)
+
+    def table(t):
+        tm = ("tm%d" % t, 16 * 10); tsp = ("ts%d" % t, 16 * 3)
+        R = [V("src")]; W = [V("tab", 0, S0)]
+        for c in range(4):
+            dma("sp", tm[0], T.tab[c::16, (3 - c) * PITCH:(19 - c) * PITCH], T.src[:, 0:PITCH], R, W, tm)
+        for c in range(1, 4):
+            for j in range(c):
+                s = 19 - c + j
+                dma("sp", tm[0], T.tab[c::16, s * PITCH:(s + 1) * PITCH], T.src[j::16, 1:PITCH + 1], R, W, tm)
+        for c in range(1, 4):
+            dma("sp", tsp[0], T.tab[c::16, S0:TABW], T.src[:, 128 * c:128 * c + 128], R, [V("tab", S0, TABW)], tsp)
+
+    def regions(share):
+        m = min(768 + share, 1536)
+        return [(0, 256), (256, 256 + share), (256 + share, m), (m, 1536), (1536, 1792), (1792, 2048)]
+
+    def gathers(win, off, dst, c0, share, between=None, op=None):
+        for n, (a, b) in enumerate(regions(share)):
+            if op is not None and n != 1:
+                out, o, z = V(dst, c0 + a, c0 + b), V(off, a // 16, b // 16), V("zr", a, b)
+                emit("dve", lambda: g.vector.tensor_tensor(out[0], win[0].indirect(o[0]), z[0], op), [win, o, z], [out])
+            else:
+                gat("act" if n == 1 else "dve", dst, c0, win, off, a, b)
+            if between and n in between: between[n]()
+
+    def sums(bank, ab, sel, p0, p1, stop=False):
+        for j in range(16):
+            mm(P(bank, j, 128, 16, p0, p1), V(ab, 16 * p0 + j, 16 * p1, 16), sel, False, stop and j == 15)
+
+    def sizes(dst, c0, ab, zpart, share, bank=None, sel=None, between=None):
+        for n, (a, b) in enumerate(regions(share)):
+            if between and n in between: between[n]()
+            o = P(n % 4, 0, b - a)
+            cur = (V("Ib"), V(dst, c0 + a, c0 + b))
+            if FUSE and zpart and n != 1:
+                act(V(ab, a, b), cur[1], F.Abs)
+                continue
+            if zpart: group(o, [(V("nzT"), V("E", a, b)), cur])
+            else: group(o, [cur, (V("nIb"), V(dst, c0 + a - 1, c0 + b - 1))])
+            act(V(ab, a, b), o, F.Abs)
+        if bank is not None:
+            sums(bank, ab, sel, 0, 96, True)
+            sums(bank, ab, sel, 96, 128, True)
+
+    def zero(o): mm(o, V("zer", 0, 128), V("m16", 0, o[3] - o[2]), True, False)
+
+    def xsizes(t, more=None):
+        b = {3: lambda: mm(P(4), V("onf", 0, 128, 1, 0, 8), V("thE", 128 * t, 128 * t + 128, 1, 0, 8), True, False)}
+        if more:
+            b[2] = more
+            b[5] = lambda: mm(P(4), V("c16", 0, 128, 1, 0, 8), V("aE", 0, 128, 1, 0, 8), False, False)
+        sizes("xb", 16, "ab2", False, GX, 4, V("grp"), b)
+
+    def blockscan(a, b):
+        scan(V("ysc", a, b), V("m16", 0, b - a), V("xb", 16 + a, 16 + b), 0.0, A.mult, A.max)
+
+    dma("sp", "dl0", T.li[:], T.l0[:], [], [V("li")])
+    dma("sp", "dx0", T.X[:, 0:2048], T.x0[:, 0:2048], [], [V("X", 0, 2048)])
+    dma("act", "dx1", T.X[:, 2048:4096], T.x0[:, 2048:4096], [], [V("X", 2048, 4096)])
+    dma("sp", "dth", T.thi[0:8, 0:3], T.th[:], [], [V("thi")])
+    dma("sp", "dz", T.za[:], T.z0[:], [], [V("za")])
+    iota(V("vb"), [[1, 128]], 0, -1)
+    iota(V("gi"), [[-16, 8]], 0, 1)
+    iota(V("stg"), [[-1, 8], [0, 16]], 0, 1)
+    iota(V("st2"), [[0, 8], [1, 16]], 0, 16)
+    iota(V("c32"), [[512, 8]], 0, 32)
+    iota(V("st3"), [[0, 8], [-384, 16]], 8576, 0)
+    ms(V("tab", 0, 2048), 0.0)
+    act(V("tab", F0, F0 + 2048), V("tab", 0, 2048), F.Copy)
+    act(V("tab", F0 + 2048, F1), V("tab", 0, F1 - F0 - 2048), F.Copy)
+    iota(V("tab", F1, S0), [[0, S0 - F1]], 0, 0)
+    iota(V("tab", S0, TABW), [[0, TABW - S0]], 0, 0)
+    ms(V("tab", 2048, F0), 0.0)
+    ts(V("Ib"), V("vb"), 0.0, None, A.is_equal)
+    ts(V("nIb"), V("vb"), 0.0, -1.0, A.is_equal, A.mult)
+    ms(V("xb", 0, 16), -1024.0)
+    ts(V("gj"), V("gi"), 4, None, A.arith_shift_right)
+    ms(V("src", 512, 528), 0.0)
+    ms(V("onf"), 1.0)
+    ts(V("Egf"), V("stg"), 0.0, None, A.is_equal)
+    ts(V("grp"), V("gj"), 0.0, None, A.is_equal)
+    cp(V("ox"), V("li"))
+    for p in range(4):
+        ts(V("dgi", 128 * p, 128 * p + 128), V("li"), 3 * (3 - p), 7, A.logical_shift_right, A.bitwise_and)
+    cp(V("thf", 0, 3, 1, 0, 8), V("thi", 0, 3, 1, 0, 8))
+    cp(V("src", 0, 512), V("dgi"))
+    def threshold(t):
+        ts(V("thE", 128 * t, 128 * t + 128, 1, 0, 8), V("Egf", 0, 128, 1, 0, 8), V("thf", t, t + 1, 1, 0, 8), -1.0, A.mult, A.mult)
+    threshold(0)
+    ms(V("onF"), 1.0); ms(V("onB"), 1.0); ms(V("c16"), 16.0); ms(V("nb"), 0.0); ms(V("zer"), 0.0)
+    ms(V("onF", 0, 128, 16), BIG); ms(V("onB", 15, 128, 16), BIG)
+    table(0)
+    ms(V("m16"), 1.0)
+    gathers(V("X"), "ox", "xb", 16, GX)
+    cp(V("EF"), V("Egf")); cp(V("EB"), V("Egf"))
+    cp(V("Ibuf"), V("zer")); cp(V("Wbuf"), V("zer"))
+    ts(V("EF", 0, 128, 1, 32, 33), V("st2", 0, 128, 1, 32, 33), -511.0, None, A.add)
+    ts(V("EB", 0, 128, 1, 32, 33), V("st2", 0, 128, 1, 32, 33), -1.0, 528.0, A.mult, A.add)
+    ts(V("Ibuf", 0, 144, 1, 32, 33), V("zer", 0, 144, 1, 32, 33), 1.0, None, A.add)
+    ts(V("Wbuf", 0, 144, 1, 32, 33), V("zer", 0, 144, 1, 32, 33), 1.0, None, A.add)
+    threshold(1); threshold(2)
+    xsizes(0)
+    act(V("kc"), V("st2"), F.Copy)
+    for s in SCALES[:11]: act(I(s), V("Ib"), F.Copy, scale=float(s))
+    act(V("dlt"), V("st3"), F.Copy)
+    act(V("s9", 0, 1), V("Ib", 112, 113), F.Copy)
+    act(V("s9", 1, 9), V("Ib", 0, 128, 16), F.Copy)
+    act(V("dlt", 0, 128, 16), V("onf", 0, 8), F.Copy, scale=385.0)
+
+    def fill(n):
+        if n == 0:
+            ts(V("gj"), V("c32"), 9, None, A.arith_shift_right)
+        if n == 1:
+            ts(V("uf", 0, 1), V("gj", 0, 1), 512.0, None, A.mult); ms(V("S"), 0.0)
+        if n == 2:
+            ms(V("m16", 0, 512, 16), 0.0); cp(V("S", 15, 143, 16), V("grp"))
+            ts(V("ui"), V("c32"), V("uf", 0, 1), None, A.subtract)
+        if n == 3:
+            for c in range(1, 3): cp(V("s24", 8 * c - 8, 8 * c), V("Ib", c, 128, 16))
+        if n == 4:
+            cp(V("s24", 16, 24), V("Ib", 3, 128, 16)); cp(V("c32"), V("ui"))
+        if n == 5:
+            for s in SCALES[11:]: ts(I(s), V("vb"), 0.0, float(s), A.is_equal, A.mult)
+        if n == 6:
+            ts(V("ngrp"), V("grp"), -1.0, None, A.mult); cp(V("onh"), V("onf", 0, 8))
+            for j in range(3): cp(V("E", j, 2048, 16), V("Ib"))
+        if n == 7:
+            for j in range(3, 8): cp(V("E", j, 2048, 16), V("Ib"))
+        if n == 8:
+            for j in range(8, 16): act(V("E", j, 2048, 16), V("Ib"), F.Copy)
+
+    zc, zn = "za", "zb"
+    Y = V("ysc", 15, 2048, 16)
+    ii, jj, kc = V("ii"), V("jj"), V("kc")
+    cs = [V("cc", 128 * n, 128 * n + 128) for n in range(3)]
+    cls = [V("cl", 128 * n, 128 * n + 128) for n in range(3)]
+    tk0, tk3 = V("tk", 0, 128), V("tk", 128, 256)
+    ta, tb = [V("ta", 128 * n, 128 * n + 128) for n in range(3)], [V("tb", 128 * n, 128 * n + 128) for n in range(3)]
+    mid = [(ta[0], I(64)), (tb[0], I(64)), (ta[1], I(8)), (tb[1], I(8))]
+    for t in range(RO):
+        d0n, d3n, hin, lwn = "d0_%d" % t, "d3_%d" % t, "hi_%d" % t, "lw_%d" % t
+        d0, d3 = V(d0n, 16, 144), V(d3n, 32, 160)
+
+        def gap(n, pieces):
+            if t == 0: fill(n)
+            else:
+                for q in pieces: blockscan(256 * q, 256 * q + 256)
+        zero(P(0, 0, 384))
+        ts(V("nb", 0, 128), P(4), 0.0, None, A.is_le)
+        scan(V("il"), V("onF"), V("nb", 0, 128), 0.0, A.add, A.mult)
+        scan(V("wl", 0, 128, -1), V("onB", 0, 128, -1), V("nb", 0, 128, -1), 0.0, A.add, A.mult)
+        group(P(7, 0, 128, 1, 0, 8), [(V("il", 15, 128, 16), V("Ib"))], last=False)
+        group(P(7, 128, 256, 1, 0, 8), [(V("wl", 0, 128, 16), V("Ib"))])
+        scan(V("jl", 0, 128, -1), V("nb", 1, 129, -1), V("onB", 0, 128, -1), 0.0, A.mult, A.add)
+        gap(0, [4])
+        scan(V("Ibuf", 1, 129, 1, 0, 8), V("c16", 0, 128, 1, 0, 8), P(7, 0, 128, 1, 0, 8), 0.0, A.add, A.min)
+        scan(V("Wbuf", 0, 128, -1, 0, 8), V("c16", 0, 128, 1, 0, 8), P(7, 128, 256, -1, 0, 8), 0.0, A.add, A.min)
+        group(P(5), [(V("Ibuf", 0, 128, 1, 0, 33), V("EF", 0, 128, 1, 0, 33))])
+        group(P(4), [(V("Wbuf", 1, 129, 1, 0, 33), V("EB", 0, 128, 1, 0, 33))])
+        tt(ii, P(5), V("il"), A.min)
+        tt(jj, P(4), V("jl"), A.min)
+        for n, a in enumerate((3, 1, 1)): mm(P(0, 128 * n, 128 * n + 128), I(a), ii, False, False)
+        for n, b in enumerate((-1, -1, -3)): mm(P(0, 128 * n, 128 * n + 128), I(b), jj, False, n == 2)
+        for n in range(3):
+            group(P(1, 128 * n, 128 * n + 128), [(I(1), ii), (I(1), jj)], last=n == 2)
+        group(P(2), [(I(1), kc), (I(3), ii)], stop=False)
+        group(P(7), [(kc, I(512)), (ii, I(1536))], stop=False)
+        group(P(6), [(I(-3), ii), (I(1), jj)], stop=False)
+        gap(1, [5])
+        ts(V("cc"), P(0, 0, 384), 0.0, None, A.is_ge)
+        group(P(7), [(c, I(128)) for c in cs], start=False, stop=False)
+        tt(V("cl"), P(1, 0, 384), V("cc"), A.mult)
+        group(P(2), [(I(-1), c) for c in cls], start=False)
+        group(P(6), [(I(1), c) for c in cls], start=False)
+        group(P(7), [(c, I(-512)) for c in cls], start=False, stop=False)
+        act(P(3, 128, 256), P(1), F.Relu, bias=32768.0, scale=-16384.0)
+        gap(2, [6])
+        ts(V("h0"), P(2), 1.0 / 16, HC, A.mult, A.add)
+        group(P(7), [(V("h0"), I(-8192)), (V("h0"), I(1))], start=False)
+        group(P(5), [(I(1), kc), (I(2), ii), (I(-1), jj)] + [(I(-1), c) for c in cls])
+        group(P(4), [(kc, I(512)), (ii, I(1024)), (jj, I(-512))] + [(c, I(-512)) for c in cls]
+              + [(c, I(128)) for c in cs], stop=False)
+        for c in range(3):
+            act(V("mm", 128 * c, 128 * c + 128), P(6), F.Relu, bias=-8.0 * (c + 1), scale=8.0)
+        tt(V("dv"), P(3, 128, 256), V("dlt"), A.min)
+        ts(V("o0"), P(7), 8191 * MAG + 3 * PITCH, None, A.add)
+        W0, W1 = V("tab", 0, S0), V("tab")
+        gat("act", "G0", 0, W0, "o0", 0, G0S)
+        gap(3, [7])
+        ts(V("h1"), P(5), 1.0 / 16, HC, A.mult, A.add)
+        gat("dve", "G0", 0, W0, "o0", G0S, 2048)
+        group(P(4), [(V("h1"), I(-8192)), (V("h1"), I(1)), (V("dv"), I(1))], start=False)
+        if t > 0:
+            for j in range(16):
+                mm(P(5, 0, 8), V("S", 15 - j, 143 - j), V("ysc", 16 * j + 15, 2048, 256), j == 0, j == 15, last=False)
+            group(P(5, 128, 256), [(V("Ib"), Y), (V("Ib"), V(zc))])
+            group(P(3), [(V("Ib"), Y), (V("nIb"), V(zc))])
+        for j in range(16):
+            mm(P(7, j, 144, 16), V("G0", j, 2048, 16), V("s9", 0, 9), True, True, last=j == 15)
+        ts(V("o1"), P(4), 8191 * MAG + 3 * PITCH + 128, None, A.add)
+        for c in range(3):
+            act(V("mb", 128 * c, 128 * c + 128), P(6), F.Relu, bias=8.0 * (c + 2), scale=-8.0)
+        if FUSE:
+            if t > 0: act(V("zsp", 0, 2048, 16), P(3), F.Abs)
+            else:
+                ms(V("zsp"), 0.0); act(V("zsp", 0, 2048, 16), V(zc), F.Copy)
+        act(V(d0n), P(7, 0, 144), F.Copy)
+        send(hop, hin if direct else "rl_%d" % t, V(d0n, 0, 128), ("ah%d" if direct else "ar%d") % t, m1)
+        if t > 0:
+            cp(V("ui"), P(5, 0, 8))
+            ts(V("zh"), P(5, 128, 256), 0.5, -0.25, A.mult, A.add)
+            ts(V("um"), V("ui"), 31, None, A.bitwise_and)
+            tt(V("uf"), V("um"), V("c32"), A.add)
+            cp(V("oc"), V("uf"))
+        else:
+            fill(4); fill(5)
+        for j in range(16):
+            mm(P(0, j, 384, 16), V("G0", j, 2048, 16), V("s24"), True, True, last=j == 15)
+        gat("act", "G1", 0, W1, "o1", 0, G1S)
+        if FUSE:
+            for n, (a, b) in enumerate(regions(GX)):
+                if n != 1: scan(V("zr", a, b), V("m16", 0, b - a), V("zsp", a, b), 0.0, A.mult, A.add)
+        gat("dve", "G1", 0, W1, "o1", G1S, 2048)
+        for j in range(16):
+            mm(P(1, j, 384, 16), V("G1", j, 2048, 16), V("s24"), True, True, last=j == 15)
+        if t > 0:
+            act(V(zn), P(3), F.Abs)
+            zc, zn = zn, zc
+        tt(V("ta"), P(0, 0, 384), V("mm"), A.min)
+        group(P(3), [(V(zc), V("nIb"))])
+        act(V("nzT"), P(3), F.Copy)
+        if t == 0: fill(8)
+        group(P(6), [(d0, I(512)), (ta[2], I(1)), mid[0], mid[2]], stop=False)
+        tt(tb[2], P(1, 256, 384), V("mb", 256, 384), A.min)
+        group(P(2, 32, 160), [(I(1), ta[2]), (I(1), tb[2])], last=False)
+        group(P(2, 0, 32), [(I(1), V("ta", 352, 384)), (I(1), V("tb", 352, 384))])
+        tt(V("tb", 0, 256), P(1, 0, 256), V("mb", 0, 256), A.min)
+        act(V(d3n), P(2, 0, 160), F.Copy)
+        send(nx2, lwn, V(d3n, 0, 128), "al%d" % t, m2)
+        group(P(6), [(tb[2], I(1)), mid[1], mid[3]], start=False)
+        group(P(5), mid, stop=False)
+        group(P(7), [(kc, I(1))], stop=False)
+        zero(P(4))
+        if t > 0:
+            emit("dve", lambda: g.vector.tensor_copy(T.X[:].indirect(T.oc[:]), T.zh[:]), [V("oc"), V("zh")], [V("X")])
+        else:
+            fill(6)
+        cp(V("oP"), P(6))
+        if t == 0: fill(7)
+        gathers(V("X"), "oP", "yy", 0, GY, None, A.subtract if FUSE else None)
+        if t < RO - 1:
+            mm(P(6, 128, 256), ta[0], I(1), True, False); mm(P(6, 128, 256), tb[0], I(1), False, False)
+            group(P(6, 256, 384), [(ta[1], I(1)), (tb[1], I(1))], start=False, stop=False)
+            mm(P(6, 0, 128), d0, I(1), False, False); mm(P(6, 384, 512), d3, I(1), False, False)
+        else:
+            group(P(6), mid + [(d0, I(512)), (d3, I(1))], stop=False)
+
+        def name_m():
+            mm(P(5), V(lwn), I(1), False, False, after=[("al%d" % t, n_lo)])
+            mm(P(5), V(hin), I(512), False, True, after=[("ah%d" % t, n_hi)])
+            cp(V("oM"), P(5))
+        sizes("yy", 0, "aby", True, GY, None, None, {5: name_m})
+        gathers(V("X"), "oM", "yy", 2048, GM, None, A.subtract if FUSE else None)
+
+        def diffs():
+            group(P(5), [(I(1), V(hin)), (I(-1), d0)], last=False)
+            group(P(5, 128, 256), [(I(1), V(lwn)), (I(-1), d3)])
+        sizes("yy", 2048, "ab2", True, GM, 4, V("grp"), {2: lambda: sums(4, "aby", V("ngrp"), 0, 128), 4: diffs})
+        ts(V("took"), P(4), 0.0, None, A.is_lt)
+        group(P(7), [(V("took"), I(2048))], start=False)
+        cp(V("ox"), P(7))
+
+        def taken():
+            tt(tk0, P(5), V("took"), A.mult)
+            tt(tk3, P(5, 128, 256), V("took"), A.mult)
+        if t < RO - 1:
+            for j in range(16):
+                mm(P(7, 256, 257, 1, 0, 8), V("took", j, 128, 16), V("onh", 0, 1), j == 0, j == 15)
+            col = lambda n: V(n, 0, 1, 1, 0, 8)
+
+            def count0():
+                cp(col("ai"), P(7, 256, 257, 1, 0, 8)); taken(); ts(col("am"), col("ai"), 31, None, A.bitwise_and)
+            gathers(V("yy"), "ox", "xb", 16, GX, {0: count0, 2: lambda: cp(col("af"), col("am")), 3: lambda: ts(
+                V("aE", 0, 128, 1, 0, 8), V("Egf", 0, 128, 1, 0, 8), col("af"), -1.0 / 16, A.mult, A.mult)},
+                A.add if FUSE else None)
+
+            def names():
+                mm(P(6, 0, 128), tk0, I(1), False, False); mm(P(6, 384, 512), tk3, I(1), False, True)
+                if EV == 0:
+                    act(V("src", 0, 512), P(6, 0, 512), F.Copy); table(t + 1)
+            blockscan(0, 512); blockscan(512, 1024)
+            xsizes(t + 1, names)
+            if EV == 1:
+                act(V("src", 0, 512), P(6, 0, 512), F.Copy); table(t + 1)
+        else:
+            def xq(a, b, e, q):
+                gat(e, "xb", 16, V("yy"), "ox", a, b)
+                dma("sp", "oxy%d" % q, T.xy[:, a:b], T.xb[:, 16 + a:16 + b], [V("xb", 16 + a, 16 + b)], [])
+            taken()
+            group(P(6), [(tk0, I(512)), (tk3, I(1))], start=False)
+            if FUSE:
+                gathers(V("yy"), "ox", "xb", 16, GX, None, A.add)
+                act(V("lo"), P(6), F.Copy)
+                dma("sp", "oly", T.ly[:], T.lo[:], [V("lo")], [])
+                for q, (a, b) in enumerate(((0, 768), (768, 1280), (1280, 1792), (1792, 2048))):
+                    dma("sp", "oxy%d" % q, T.xy[:, a:b], T.xb[:, 16 + a:16 + b], [V("xb", 16 + a, 16 + b)], [])
+                for q in range(4): blockscan(512 * q, 512 * q + 512)
+            else:
+                xq(0, 640, "act", 0); xq(640, 1152, "dve", 1)
+                act(V("lo"), P(6), F.Copy)
+                dma("sp", "oly", T.ly[:], T.lo[:], [V("lo")], [])
+                xq(1152, 1664, "act", 2); xq(1664, 2048, "act", 3)
+                blockscan(0, 512); blockscan(512, 1024); blockscan(1024, 1152); blockscan(1152, 1664); blockscan(1664, 2048)
+            group(P(3), [(V("Ib"), Y), (V("nIb"), V(zc))])
+            act(V(zn), P(3), F.Abs)
+            dma("act", "ozy", T.zy[:], T[zn][:], [V(zn)], [])
+    for s in ["pe", "dve", "act", "pool"] + DSEMS:
+        if cnt.get(s, 0): g.wait_ge(T.sem[s], cnt[s])
+    g.wait_ge(T.sem.sent, sent[0])

@@ -5,46 +5,58 @@ PITCH = 512
 S0 = 19 * PITCH
 TABW = S0 + 2048
 BIG = 4096.0
-MAG = 1536.0
+MAG = 1088.0
 HC = MAG - 7.5 / 16
+M32 = 49152.0
+ND = 72
+NX = 80
+NL = 72
+G0S, G1S = 960, 832
+F0, F1, F2 = 3072, 6656, 9728
 
 bf, f16, f32, i32, u16 = "bfloat16", "float16", "float32", "int32", "uint16"
 SB = {
     "X": (4096, bf), "tab": (TABW, bf), "xb": (2064, bf), "yy": (4096, bf), "aby": (2048, bf), "ab2": (2048, bf),
-    "G0": (2048, bf), "G1": (2048, bf), "ysc": (2048, bf), "E": (2048, bf), "zr": (2048, bf), "zsp": (2048, bf), "m16": (512, bf),
+    "mx": (2048, bf), "G0": (2048, bf), "G1": (2048, bf), "ysc": (2048, bf), "nE": (2048 - 16 * ND, bf), "zr": (2048, bf),
+    "zsp": (2048, bf), "m16": (1280, bf), "m8": (1024, bf),
     "li": (128, i32), "dgi": (512, i32), "src": (528, bf), "thi": (4, i32), "thf": (4, f32),
-    "za": (128, bf), "zb": (128, bf), "nzT": (128, bf), "zh": (128, i32),
+    "za": (128, bf), "zT": (128, bf), "zh": (128, i32), "zo": (128, bf),
     "ox": (128, u16), "o0": (128, u16), "o1": (128, u16), "oP": (128, u16), "oM": (128, u16), "oc": (8, u16),
-    "ui": (8, i32), "um": (8, i32), "uf": (8, f32), "c32": (8, i32),
-    "ai": (4, i32), "am": (4, i32), "af": (4, f32), "thE": (384, f32), "aE": (128, bf), "Egf": (128, f32), "onf": (128, f32),
+    "uf": (8, f32), "c32": (8, i32),
+    "thE": (384, f32), "Egf": (128, f32), "onf": (128, f32),
     "vb": (128, bf), "stg": (128, f32), "st2": (128, f32), "st3": (128, f32), "gi": (8, i32), "gj": (8, i32),
-    "Ib": (128, bf), "nIb": (128, bf), "grp": (8, bf), "ngrp": (8, bf), "S": (144, bf), "s9": (16, bf), "s24": (24, bf),
-    "zer": (144, bf), "onF": (128, bf), "onB": (128, bf), "c16": (128, bf),
-    "kc": (128, f16), "dlt": (128, f16), "EF": (128, f16), "EB": (128, f16), "onh": (8, f16),
-    "nb": (144, bf), "il": (128, bf), "jl": (128, bf), "wl": (128, bf), "Ibuf": (144, f16), "Wbuf": (144, f16),
-    "ii": (128, f16), "jj": (128, f16), "cc": (384, f16), "cl": (384, f16), "h0": (128, f16), "h1": (128, f16),
-    "dv": (128, f16), "n3": (384, f16), "mm": (384, f16), "mb": (384, f16),
-    "ta": (384, f16), "tb": (384, f16), "took": (128, f16), "tk": (256, f16), "lo": (128, f32),
+    "Ib": (128, bf), "nIb": (128, bf), "ngrp": (8, bf), "grp2": (8, bf), "s32": (32, bf),
+    "s26": (32, bf), "c16": (128, bf), "c24": (128, f16), "jF": (128, bf), "jB": (128, bf),
+    "ZB": (160, bf), "ZF": (264, f32), "ZH": (416, f16), "OB": (256, bf),
+    "GGb": (128, bf), "qm": (128, f16), "sel": (8, f16), "c32h": (8, f16),
+    "kc": (128, f16), "dlt": (128, f16), "Eg": (128, f16), "onh": (128, f16), "GG": (128, f16), "nGG": (128, f16),
+    "il": (128, bf), "jl": (128, bf), "wl": (128, bf),
+    "ii": (128, f16), "jj": (128, f16), "cc": (384, f16), "cv": (384, f16), "h0": (128, f16), "h1": (128, f16),
+    "dv": (128, f16), "mk": (384, f16), "ta": (416, f16), "took": (128, f16), "rl": (256, f16), "CS": (128, f16),
+    "hA": (128, f16), "lo": (128, f32),
 }
-SCALES = [1, -1, 3, -3, 512, 1536, 128, -512, -8192, 2, 1024, 8, 64, 2048]
+PART = {"nb": ("ZB", 0, 144), "g9": ("ZB", 144, 9), "grp": ("ZB", 145, 8), "Tt": ("ZF", 0, 128), "Ssh": ("ZF", 128, 136),
+        "Ibuf": ("ZH", 0, 144), "Wbuf": ("ZH", 144, 144), "zer": ("ZH", 288, 128), "onF": ("OB", 0, 128), "onB": ("OB", 128, 128)}
+R512 = 1.0 / 512
+SCALES = [1, 3, -1, -3, 2048, -16, 2, R512, 512, 64, 8, -8208]
+
+
+def iname(s):
+    return "Ir" if s == R512 else "I%s%d" % ("m" if s < 0 else "", abs(s))
+
+
 for _s in SCALES:
-    SB["I%s%d" % ("m" if _s < 0 else "", abs(_s))] = (128, f16)
+    SB[iname(_s)] = (128, f16)
 for _t in range(RO):
-    SB["d0_%d" % _t] = (144, f16); SB["d3_%d" % _t] = (160, f16)
+    SB["d0_%d" % _t] = (144, f16); SB["dg_%d" % _t] = (416, f16)
     SB["hi_%d" % _t] = (128, f16); SB["lw_%d" % _t] = (128, f16); SB["rl_%d" % _t] = (128, f16)
 SCRATCH = {k: ("sbuf", [128, w], d) for k, (w, d) in SB.items()}
 for _b in range(8):
     SCRATCH["P%d" % _b] = ("psum", [128, 512], f32)
-DSEMS = ["dl0", "dth", "dz", "dx0", "dx1", "oly", "ozy"] + ["oxy%d" % q for q in range(4)] \
+DSEMS = ["dl0", "dth", "dz", "dx0", "dx1", "dfl", "dfe", "oly", "ozy"] + ["oxy%d" % q for q in range(4)] \
     + ["tm%d" % t for t in range(RO)] + ["ts%d" % t for t in range(RO)]
 SEMAPHORES = ["pe", "dve", "act", "pool", "sent"] + DSEMS \
     + ["ah%d" % t for t in range(RO)] + ["al%d" % t for t in range(RO)] + ["ar%d" % t for t in range(RO)]
-
-F0, F1 = 3584, 7680
-GX, GY, GM = 512, 512, 256
-G0S, G1S = 1088, 1024
-EV = 1
-FUSE = 0
 
 
 def relay_of(src, dst, topo):
@@ -77,6 +89,9 @@ def rank_program(g, core, T, topo):
     def psum(name): return name[0] == "P" and name[1:].isdigit()
 
     def V(name, c0=None, c1=None, st=1, p0=0, p1=128):
+        if name in PART:
+            b, o, w = PART[name]
+            return V(b, o + (c0 or 0), o + (w if c0 is None else c1), st, p0, p1)
         if c0 is None: c0, c1 = 0, (512 if psum(name) else SB[name][0])
         if st == 1: ap = T[name][p0:p1, c0:c1]
         elif st > 0: ap = T[name][p0:p1, c0:c1:st]
@@ -157,8 +172,11 @@ def rank_program(g, core, T, topo):
         return emit("dve", lambda: g.vector.tensor_tensor_scan(out[0], d0[0], d1[0], init, op0, op1), [d0, d1], [out])
     def act(out, a, f, bias=0.0, scale=1.0):
         return emit("act", lambda: g.scalar.activation(out[0], a[0], f, bias=bias, scale=scale), [a], [out])
-    def gat(q, name, c0, win, off, a, b):
+    def gat(q, name, c0, win, off, a, b, op=None):
         out, o = V(name, c0 + a, c0 + b), V(off, a // 16, b // 16)
+        if op is not None:
+            z = V("zr", a, b)
+            return emit(q, lambda: g.vector.tensor_tensor(out[0], win[0].indirect(o[0]), z[0], op), [win, o, z], [out])
         if q == "dve":
             return emit(q, lambda: g.vector.tensor_copy(out[0], win[0].indirect(o[0])), [win, o], [out])
         return emit(q, lambda: g.scalar.activation(out[0], win[0].indirect(o[0]), F.Copy), [win, o], [out])
@@ -168,7 +186,7 @@ def rank_program(g, core, T, topo):
         return emit("pool", lambda: g.iota(out[0], pat, base, cm, allow_small_or_imprecise_dtypes=True), [], [out])
     def dma(q, sem, out, in_, R, W, grp_tok=None):
         return emit(q, lambda: Q[q].dma_start(out, in_), R, W, sem=sem, grp_tok=grp_tok)
-    def I(s): return V("I%s%d" % ("m" if s < 0 else "", abs(s)))
+    def I(s): return V(iname(s))
     def P(b, c0=0, c1=128, st=1, p0=0, p1=128): return V("P%d" % b, c0, c1, st, p0, p1)
 
     nxt, nx2, prv = cores[(rank + 1) % N], cores[(rank + 2) % N], cores[(rank - 1) % N]
@@ -184,7 +202,7 @@ def rank_program(g, core, T, topo):
     def send(dst, name, buf, sem, mask):
         rid, pid = topo.addr(dst, core)
         for e in hist.get(buf[1], []):
-            if e[2]: wait("pool", e[4])
+            if e[2] and e[0] < buf[3] and buf[2] < e[1]: wait("pool", e[4])
         g.remote_dma(T[name][:], buf[0], T.sem[sem], T.sem.sent, pid, rid, mask)
         sent[0] += nbits(mask)
 
@@ -200,310 +218,296 @@ def rank_program(g, core, T, topo):
         for c in range(1, 4):
             dma("sp", tsp[0], T.tab[c::16, S0:TABW], T.src[:, 128 * c:128 * c + 128], R, [V("tab", S0, TABW)], tsp)
 
-    def regions(share):
-        m = min(768 + share, 1536)
-        return [(0, 256), (256, 256 + share), (256 + share, m), (m, 1536), (1536, 1792), (1792, 2048)]
+    def halves(nb):
+        a = 16 * nb; m = a + (128 - nb) // 2 * 16
+        return [(a, m), (m, 2048)]
 
-    def gathers(win, off, dst, c0, share, between=None, op=None):
-        for n, (a, b) in enumerate(regions(share)):
-            if op is not None and n != 1:
-                out, o, z = V(dst, c0 + a, c0 + b), V(off, a // 16, b // 16), V("zr", a, b)
-                emit("dve", lambda: g.vector.tensor_tensor(out[0], win[0].indirect(o[0]), z[0], op), [win, o, z], [out])
-            else:
-                gat("act" if n == 1 else "dve", dst, c0, win, off, a, b)
-            if between and n in between: between[n]()
-
-    def sums(bank, ab, sel, p0, p1, stop=False):
+    def sums(bank, buf, c0, sel, p1=128, stop=False, p0=0):
         for j in range(16):
-            mm(P(bank, j, 128, 16, p0, p1), V(ab, 16 * p0 + j, 16 * p1, 16), sel, False, stop and j == 15)
+            mm(P(bank, j, 128, 16, p0, p1), V(buf, c0 + 16 * p0 + j, c0 + 16 * p1, 16), sel, False, stop and j == 15)
 
-    def sizes(dst, c0, ab, zpart, share, bank=None, sel=None, between=None):
-        for n, (a, b) in enumerate(regions(share)):
-            if between and n in between: between[n]()
-            o = P(n % 4, 0, b - a)
-            cur = (V("Ib"), V(dst, c0 + a, c0 + b))
-            if FUSE and zpart and n != 1:
-                act(V(ab, a, b), cur[1], F.Abs)
-                continue
-            if zpart: group(o, [(V("nzT"), V("E", a, b)), cur])
-            else: group(o, [cur, (V("nIb"), V(dst, c0 + a - 1, c0 + b - 1))])
-            act(V(ab, a, b), o, F.Abs)
-        if bank is not None:
-            sums(bank, ab, sel, 0, 96, True)
-            sums(bank, ab, sel, 96, 128, True)
+    def zdist(c0, off, ab, pre=None):
+        hs = halves(ND)
+        gat("dve", "yy", c0, V("X"), off, 0, 16 * ND, A.subtract)
+        for a, b in hs: gat("act", "yy", c0, V("X"), off, a, b)
+        ts(V(ab, 0, 16 * ND), V("yy", c0, c0 + 16 * ND), 0.0, 2.0, A.max, A.mult)
+        if pre: pre()
+        for n, (a, b) in enumerate(hs):
+            group(P(n, 0, b - a), [(V("zT"), V("nE", a - 16 * ND, b - 16 * ND)), (V("Ib"), V("yy", c0 + a, c0 + b))])
+            act(V(ab, a, b), P(n, 0, b - a), F.Abs)
 
-    def zero(o): mm(o, V("zer", 0, 128), V("m16", 0, o[3] - o[2]), True, False)
+    def xdiffs(t, win, op, mid=None, mid2=None):
+        hs = halves(NX)[::-1]
+        gat("dve", "xb", 16, win, "ox", 0, 16 * NX, op)
+        for a, b in hs: gat("act", "xb", 16, win, "ox", a, b)
+        scan(V("mx", 0, 16 * NX), V("xb", 15, 15 + 16 * NX), V("xb", 16, 16 + 16 * NX), 1024.0, A.min, A.max)
+        mm(P(4), V("onf", 0, 128, 1, 0, 8), V("thE", 128 * t, 128 * t + 128, 1, 0, 8), True, False)
+        if mid: mid()
+        for n, (a, b) in enumerate(hs):
+            group(P(n, 0, b - a), [(V("Ib"), V("xb", 16 + a, 16 + b)), (V("nIb"), V("xb", 15 + a, 15 + b))])
+            act(V("mx", a, b), P(n, 0, b - a), F.Abs, scale=0.5)
+            if n == 0 and mid2: mid2()
+        for j in range(16):
+            mm(P(7, j, 128, 16, 0, NX), V("xb", 16 + j, 16 + 16 * NX, 16), V("g9", 1, 9), True, True, last=j == 15)
+        cp(V("Ssh", 1, 129, 1, 0, NX), P(7, 0, 128, 1, 0, NX))
+        tt(V("Tt", 0, 128, 1, 0, NX), P(7, 0, 128, 1, 0, NX), V("Ssh", 0, 128, 1, 0, NX), A.add)
+        mm(P(4, 0, 128, 16, 0, NX), V("xb", 31, 16 + 16 * NX, 16), V("g9", 0, 8), False, False)
+        mm(P(4, 0, 128, 16, 0, NX), V("xb", 15, 15 + 16 * NX, 16), V("ngrp"), False, False)
 
-    def xsizes(t, more=None):
-        b = {3: lambda: mm(P(4), V("onf", 0, 128, 1, 0, 8), V("thE", 128 * t, 128 * t + 128, 1, 0, 8), True, False)}
-        if more:
-            b[2] = more
-            b[5] = lambda: mm(P(4), V("c16", 0, 128, 1, 0, 8), V("aE", 0, 128, 1, 0, 8), False, False)
-        sizes("xb", 16, "ab2", False, GX, 4, V("grp"), b)
+    def xsums(): sums(4, "mx", 0, V("grp2"), 128, True)
+
+    def blockmax(n):
+        if n == 0: scan(V("ysc", 1, 16 * NX, 2), V("m8", 0, 8 * NX), V("mx", 1, 16 * NX, 2), 0.0, A.mult, A.max)
+        else: blockscan(*halves(NX)[n - 1])
 
     def blockscan(a, b):
         scan(V("ysc", a, b), V("m16", 0, b - a), V("xb", 16 + a, 16 + b), 0.0, A.mult, A.max)
 
     dma("sp", "dl0", T.li[:], T.l0[:], [], [V("li")])
+    dma("sp", "dth", T.thi[0:8, 0:3], T.th[:], [], [V("thi")])
     dma("sp", "dx0", T.X[:, 0:2048], T.x0[:, 0:2048], [], [V("X", 0, 2048)])
     dma("act", "dx1", T.X[:, 2048:4096], T.x0[:, 2048:4096], [], [V("X", 2048, 4096)])
-    dma("sp", "dth", T.thi[0:8, 0:3], T.th[:], [], [V("thi")])
     dma("sp", "dz", T.za[:], T.z0[:], [], [V("za")])
     iota(V("vb"), [[1, 128]], 0, -1)
     iota(V("gi"), [[-16, 8]], 0, 1)
     iota(V("stg"), [[-1, 8], [0, 16]], 0, 1)
     iota(V("st2"), [[0, 8], [1, 16]], 0, 16)
-    iota(V("c32"), [[512, 8]], 0, 32)
     iota(V("st3"), [[0, 8], [-384, 16]], 8576, 0)
-    ms(V("tab", 0, 2048), 0.0)
-    act(V("tab", F0, F0 + 2048), V("tab", 0, 2048), F.Copy)
-    act(V("tab", F0 + 2048, F1), V("tab", 0, F1 - F0 - 2048), F.Copy)
-    iota(V("tab", F1, S0), [[0, S0 - F1]], 0, 0)
-    iota(V("tab", S0, TABW), [[0, TABW - S0]], 0, 0)
-    ms(V("tab", 2048, F0), 0.0)
+    iota(V("jF"), [[0, 8], [1, 16]], 1, 0)
+    iota(V("jB"), [[0, 8], [-1, 16]], 16, 0)
+    ms(V("tab", 0, 1024), 0.0)
+    for a in range(F0, F1, 1024): act(V("tab", a, min(a + 1024, F1)), V("tab", 0, min(1024, F1 - a)), F.Copy)
+    iota(V("tab", F2, TABW), [[0, TABW - F2]], 0, 0)
+    iota(V("c32"), [[512, 8]], 0, 32)
+    ms(V("tab", 1024, F0), 0.0)
+    dma("sp", "dfl", T.tab[:, F1:F2], T.tab[:, 0:F2 - F1], [V("tab", 0, F2 - F1), V("X")], [V("tab", F1, F2)])
+    dma("sp", "dfe", T.nE[:], T.tab[:, 0:2048 - 16 * ND], [V("tab", 0, 2048 - 16 * ND), V("X")], [V("nE")])
     ts(V("Ib"), V("vb"), 0.0, None, A.is_equal)
     ts(V("nIb"), V("vb"), 0.0, -1.0, A.is_equal, A.mult)
-    ms(V("xb", 0, 16), -1024.0)
     ts(V("gj"), V("gi"), 4, None, A.arith_shift_right)
-    ms(V("src", 512, 528), 0.0)
-    ms(V("onf"), 1.0)
-    ts(V("Egf"), V("stg"), 0.0, None, A.is_equal)
+    ms(V("ZB"), 0.0); ms(V("ZF"), 0.0); ms(V("ZH"), 0.0); ms(V("xb", 0, 16), -1024.0); ms(V("onf"), 1.0)
     ts(V("grp"), V("gj"), 0.0, None, A.is_equal)
+    ts(V("ngrp"), V("gj"), 0.0, -1.0, A.is_equal, A.mult)
+    ts(V("grp2"), V("gj"), 0.0, 2.0, A.is_equal, A.mult)
+    ts(V("Egf"), V("stg"), 0.0, None, A.is_equal)
     cp(V("ox"), V("li"))
-    for p in range(4):
-        ts(V("dgi", 128 * p, 128 * p + 128), V("li"), 3 * (3 - p), 7, A.logical_shift_right, A.bitwise_and)
     cp(V("thf", 0, 3, 1, 0, 8), V("thi", 0, 3, 1, 0, 8))
-    cp(V("src", 0, 512), V("dgi"))
     def threshold(t):
         ts(V("thE", 128 * t, 128 * t + 128, 1, 0, 8), V("Egf", 0, 128, 1, 0, 8), V("thf", t, t + 1, 1, 0, 8), -1.0, A.mult, A.mult)
     threshold(0)
-    ms(V("onF"), 1.0); ms(V("onB"), 1.0); ms(V("c16"), 16.0); ms(V("nb"), 0.0); ms(V("zer"), 0.0)
+    ms(V("src", 512, 528), 0.0); ms(V("OB"), 1.0); ms(V("c16"), 16.0); ms(V("onh"), 1.0)
     ms(V("onF", 0, 128, 16), BIG); ms(V("onB", 15, 128, 16), BIG)
+
+    def digits():
+        for p in range(4):
+            ts(V("dgi", 128 * p, 128 * p + 128), V("li"), 3 * (3 - p), 7, A.logical_shift_right, A.bitwise_and)
+    xdiffs(0, V("X"), None, digits)
+    cp(V("src", 0, 512), V("dgi"))
     table(0)
-    ms(V("m16"), 1.0)
-    gathers(V("X"), "ox", "xb", 16, GX)
-    cp(V("EF"), V("Egf")); cp(V("EB"), V("Egf"))
-    cp(V("Ibuf"), V("zer")); cp(V("Wbuf"), V("zer"))
-    ts(V("EF", 0, 128, 1, 32, 33), V("st2", 0, 128, 1, 32, 33), -511.0, None, A.add)
-    ts(V("EB", 0, 128, 1, 32, 33), V("st2", 0, 128, 1, 32, 33), -1.0, 528.0, A.mult, A.add)
-    ts(V("Ibuf", 0, 144, 1, 32, 33), V("zer", 0, 144, 1, 32, 33), 1.0, None, A.add)
-    ts(V("Wbuf", 0, 144, 1, 32, 33), V("zer", 0, 144, 1, 32, 33), 1.0, None, A.add)
-    threshold(1); threshold(2)
-    xsizes(0)
+    emit("pool", lambda: g.affine_select(T.nE[:], T.nE[:], [[1, 128 - ND], [0, 16]], A.not_equal, -1.0, ND, -1), [V("nE")], [V("nE")])
+    act(V("Eg"), V("Egf"), F.Copy)
+    xsums()
+    group(P(3), [(V("Eg", 0, 128, 1, 0, 8), V("Eg", 0, 128, 1, 0, 8))])
     act(V("kc"), V("st2"), F.Copy)
-    for s in SCALES[:11]: act(I(s), V("Ib"), F.Copy, scale=float(s))
-    act(V("dlt"), V("st3"), F.Copy)
-    act(V("s9", 0, 1), V("Ib", 112, 113), F.Copy)
-    act(V("s9", 1, 9), V("Ib", 0, 128, 16), F.Copy)
-    act(V("dlt", 0, 128, 16), V("onf", 0, 8), F.Copy, scale=385.0)
+    act(V("dlt"), V("st3"), F.Copy, scale=1.0 / 1024)
+    act(V("dlt", 0, 128, 16), V("onf", 0, 8), F.Copy, scale=385.0 / 1024)
+    act(I(1), V("Ib"), F.Copy)
+    act(V("GG"), P(3), F.Copy); act(V("nGG"), P(3), F.Copy, scale=-1.0); act(V("GGb"), P(3), F.Copy)
+    for s in SCALES[1:8]: act(I(s), V("Ib"), F.Copy, scale=float(s))
 
     def fill(n):
         if n == 0:
-            ts(V("gj"), V("c32"), 9, None, A.arith_shift_right)
+            ms(V("m16", 0, 768), 1.0)
         if n == 1:
-            ts(V("uf", 0, 1), V("gj", 0, 1), 512.0, None, A.mult); ms(V("S"), 0.0)
+            ms(V("m16", 768, 1280), 1.0); ms(V("m16", 0, 1280, 16), 0.0)
+            for c in range(4): act(V("s32", 8 * c, 8 * c + 8), V("Ib", c, 128, 16), F.Copy)
         if n == 2:
-            ms(V("m16", 0, 512, 16), 0.0); cp(V("S", 15, 143, 16), V("grp"))
-            ts(V("ui"), V("c32"), V("uf", 0, 1), None, A.subtract)
+            ms(V("zsp", 0, 576), 0.0)
         if n == 3:
-            for c in range(1, 3): cp(V("s24", 8 * c - 8, 8 * c), V("Ib", c, 128, 16))
+            act(V("s26", 0, 16), V("s32", 8, 24), F.Copy)
+            act(V("s26", 18, 26), V("s32", 24, 32), F.Copy)
+            act(V("s26", 16, 18), V("s32", 30, 32), F.Copy)
         if n == 4:
-            cp(V("s24", 16, 24), V("Ib", 3, 128, 16)); cp(V("c32"), V("ui"))
+            ms(V("zsp", 576, 16 * ND), 0.0); cp(V("zsp", 0, 2048, 16), V("za"))
+            for s in SCALES[8:11]: ts(I(s), V("vb"), 0.0, float(s), A.is_equal, A.mult)
         if n == 5:
-            for s in SCALES[11:]: ts(I(s), V("vb"), 0.0, float(s), A.is_equal, A.mult)
+            ms(V("zr", 16 * ND, 16 * max(NX, NL, ND + 1)), 0.0)
+            ts(V("gj"), V("c32"), 9, None, A.arith_shift_right)
+            ts(V("thf", 1, 3, 1, 0, 8), V("thf", 1, 3, 1, 0, 8), M32, None, A.add)
         if n == 6:
-            ts(V("ngrp"), V("grp"), -1.0, None, A.mult); cp(V("onh"), V("onf", 0, 8))
-            for j in range(3): cp(V("E", j, 2048, 16), V("Ib"))
+            threshold(1); cp(V("sel"), V("grp"))
+            ts(V("uf", 0, 1), V("gj", 0, 1), 512.0, None, A.mult)
         if n == 7:
-            for j in range(3, 8): cp(V("E", j, 2048, 16), V("Ib"))
+            ms(V("m8", 0, 8 * NX), 1.0); ms(V("c24"), M32 / 2048)
+            ts(V("c32h"), V("c32"), V("uf", 0, 1), None, A.subtract)
+            ms(V("m8", 0, 8 * NX, 8), 0.0)
+            ts(V("uf", 1, 2), V("c32h", 0, 1), 1.0 / 32, V("st2", 0, 1), A.mult, A.add)
         if n == 8:
-            for j in range(8, 16): act(V("E", j, 2048, 16), V("Ib"), F.Copy)
+            ts(V("qm"), V("st2"), V("uf", 1, 2), None, A.is_equal)
+            threshold(2); ts(I(-8208), V("vb"), 0.0, -8208.0, A.is_equal, A.mult)
 
-    zc, zn = "za", "zb"
-    Y = V("ysc", 15, 2048, 16)
-    ii, jj, kc = V("ii"), V("jj"), V("kc")
+    Y, Z = V("ysc", 15, 2048, 16), V("zsp", 0, 2048, 16)
+    ii, jj, kc, took = V("ii"), V("jj"), V("kc"), V("took")
     cs = [V("cc", 128 * n, 128 * n + 128) for n in range(3)]
-    cls = [V("cl", 128 * n, 128 * n + 128) for n in range(3)]
-    tk0, tk3 = V("tk", 0, 128), V("tk", 128, 256)
-    ta, tb = [V("ta", 128 * n, 128 * n + 128) for n in range(3)], [V("tb", 128 * n, 128 * n + 128) for n in range(3)]
-    mid = [(ta[0], I(64)), (tb[0], I(64)), (ta[1], I(8)), (tb[1], I(8))]
+    cv = [V("cv", 128 * n, 128 * n + 128) for n in range(3)]
+    mk = [V("mk", 128 * n, 128 * n + 128) for n in range(3)]
     for t in range(RO):
-        d0n, d3n, hin, lwn = "d0_%d" % t, "d3_%d" % t, "hi_%d" % t, "lw_%d" % t
-        d0, d3 = V(d0n, 16, 144), V(d3n, 32, 160)
+        d0n, dgn, hin, lwn = "d0_%d" % t, "dg_%d" % t, "hi_%d" % t, "lw_%d" % t
+        d0, d1, d2, d3 = V(d0n, 16, 144), V(dgn, 0, 128), V(dgn, 128, 256), V(dgn, 288, 416)
 
-        def gap(n, pieces):
+        def gap(n):
             if t == 0: fill(n)
-            else:
-                for q in pieces: blockscan(256 * q, 256 * q + 256)
-        zero(P(0, 0, 384))
-        ts(V("nb", 0, 128), P(4), 0.0, None, A.is_le)
+            elif n < 3: blockmax(n)
+        tt(V("nb", 0, 128), P(4), V("Tt"), A.is_le)
         scan(V("il"), V("onF"), V("nb", 0, 128), 0.0, A.add, A.mult)
         scan(V("wl", 0, 128, -1), V("onB", 0, 128, -1), V("nb", 0, 128, -1), 0.0, A.add, A.mult)
-        group(P(7, 0, 128, 1, 0, 8), [(V("il", 15, 128, 16), V("Ib"))], last=False)
-        group(P(7, 128, 256, 1, 0, 8), [(V("wl", 0, 128, 16), V("Ib"))])
+        group(P(7, 0, 128, 1, 0, 8), [(V("il", 15, 128, 16), V("Ib"))])
+        group(P(0, 0, 128, 1, 0, 8), [(V("wl", 0, 128, 16), V("Ib"))])
         scan(V("jl", 0, 128, -1), V("nb", 1, 129, -1), V("onB", 0, 128, -1), 0.0, A.mult, A.add)
-        gap(0, [4])
+        group(P(3), [(I(1), V("dlt"))], stop=False)
+        group(P(4), [(kc, I(1))], stop=False)
+        group(P(5), [(V("Ib"), V("jF"))], stop=False)
+        group(P(6), [(V("Ib"), V("jB"))], stop=False)
         scan(V("Ibuf", 1, 129, 1, 0, 8), V("c16", 0, 128, 1, 0, 8), P(7, 0, 128, 1, 0, 8), 0.0, A.add, A.min)
-        scan(V("Wbuf", 0, 128, -1, 0, 8), V("c16", 0, 128, 1, 0, 8), P(7, 128, 256, -1, 0, 8), 0.0, A.add, A.min)
-        group(P(5), [(V("Ibuf", 0, 128, 1, 0, 33), V("EF", 0, 128, 1, 0, 33))])
-        group(P(4), [(V("Wbuf", 1, 129, 1, 0, 33), V("EB", 0, 128, 1, 0, 33))])
+        scan(V("Wbuf", 0, 128, -1, 0, 8), V("c16", 0, 128, 1, 0, 8), P(0, 0, 128, -1, 0, 8), 0.0, A.add, A.min)
+        group(P(5), [(V("Ibuf", 0, 128, 1, 0, 8), V("Eg", 0, 128, 1, 0, 8))], start=False)
+        group(P(7), [(kc, I(1))], stop=False)
+        group(P(6), [(V("Wbuf", 1, 129, 1, 0, 8), V("Eg", 0, 128, 1, 0, 8))], start=False)
+        group(P(2), [(I(1), kc)], stop=False)
+        for n in range(3): mm(P(1, 128 * n, 128 * n + 128), I(2048), V("onh"), n == 0, False)
         tt(ii, P(5), V("il"), A.min)
-        tt(jj, P(4), V("jl"), A.min)
-        for n, a in enumerate((3, 1, 1)): mm(P(0, 128 * n, 128 * n + 128), I(a), ii, False, False)
+        tt(jj, P(6), V("jl"), A.min)
+        for n, a in enumerate((3, 1, 1)): mm(P(0, 128 * n, 128 * n + 128), I(a), ii, n == 0, False)
         for n, b in enumerate((-1, -1, -3)): mm(P(0, 128 * n, 128 * n + 128), I(b), jj, False, n == 2)
         for n in range(3):
-            group(P(1, 128 * n, 128 * n + 128), [(I(1), ii), (I(1), jj)], last=n == 2)
-        group(P(2), [(I(1), kc), (I(3), ii)], stop=False)
-        group(P(7), [(kc, I(512)), (ii, I(1536))], stop=False)
-        group(P(6), [(I(-3), ii), (I(1), jj)], stop=False)
-        gap(1, [5])
+            group(P(1, 128 * n, 128 * n + 128), [(I(-1), ii), (I(-1), jj)], start=False, stop=n == 2)
+        group(P(2), [(I(3), ii)], start=False, stop=False)
+        group(P(7), [(ii, I(3))], start=False, stop=False)
+        group(P(3), [(I(-16), ii), (I(-16), jj)], start=False)
+        group(P(5), [(I(1), kc), (I(2), ii), (I(-1), jj)], stop=False)
+        group(P(4), [(ii, I(2)), (jj, I(-1))], start=False, stop=False)
+        gap(0)
         ts(V("cc"), P(0, 0, 384), 0.0, None, A.is_ge)
-        group(P(7), [(c, I(128)) for c in cs], start=False, stop=False)
-        tt(V("cl"), P(1, 0, 384), V("cc"), A.mult)
-        group(P(2), [(I(-1), c) for c in cls], start=False)
-        group(P(6), [(I(1), c) for c in cls], start=False)
-        group(P(7), [(c, I(-512)) for c in cls], start=False, stop=False)
-        act(P(3, 128, 256), P(1), F.Relu, bias=32768.0, scale=-16384.0)
-        gap(2, [6])
+        tt(V("cv"), P(1, 0, 384), V("cc"), A.mult)
+        act(V("dv"), P(3), F.Relu, bias=32.0, scale=2.0)
+        group(P(2), [(I(1), c) for c in cv], start=False)
+        group(P(5), [(I(1), c) for c in cv], start=False)
+        group(P(7), [(c, I(1)) for c in cv], start=False, stop=False)
+        gap(1)
         ts(V("h0"), P(2), 1.0 / 16, HC, A.mult, A.add)
-        group(P(7), [(V("h0"), I(-8192)), (V("h0"), I(1))], start=False)
-        group(P(5), [(I(1), kc), (I(2), ii), (I(-1), jj)] + [(I(-1), c) for c in cls])
-        group(P(4), [(kc, I(512)), (ii, I(1024)), (jj, I(-512))] + [(c, I(-512)) for c in cls]
-              + [(c, I(128)) for c in cs], stop=False)
-        for c in range(3):
-            act(V("mm", 128 * c, 128 * c + 128), P(6), F.Relu, bias=-8.0 * (c + 1), scale=8.0)
-        tt(V("dv"), P(3, 128, 256), V("dlt"), A.min)
-        ts(V("o0"), P(7), 8191 * MAG + 3 * PITCH, None, A.add)
+        group(P(7), [(V("h0"), I(-16)), (V("h0"), I(R512))], start=False)
+        act(V("h1"), P(5), F.Identity, bias=HC + 128, scale=1.0 / 16)
+        group(P(4), [(c, I(1)) for c in cv] + [(V("dv"), I(1)), (V("h1"), I(-16)), (V("h1"), I(R512))], start=False)
+        group(P(6), [(I(1), jj), (I(-3), ii)] + [(I(2048), c) for c in cs] + [(I(-1), c) for c in cv])
+        gap(2)
+        ts(V("o0"), P(7), 512.0, 8191 * MAG + 3 * PITCH, A.mult, A.add)
         W0, W1 = V("tab", 0, S0), V("tab")
         gat("act", "G0", 0, W0, "o0", 0, G0S)
-        gap(3, [7])
-        ts(V("h1"), P(5), 1.0 / 16, HC, A.mult, A.add)
         gat("dve", "G0", 0, W0, "o0", G0S, 2048)
-        group(P(4), [(V("h1"), I(-8192)), (V("h1"), I(1)), (V("dv"), I(1))], start=False)
         if t > 0:
-            for j in range(16):
-                mm(P(5, 0, 8), V("S", 15 - j, 143 - j), V("ysc", 16 * j + 15, 2048, 256), j == 0, j == 15, last=False)
-            group(P(5, 128, 256), [(V("Ib"), Y), (V("Ib"), V(zc))])
-            group(P(3), [(V("Ib"), Y), (V("nIb"), V(zc))])
-        for j in range(16):
-            mm(P(7, j, 144, 16), V("G0", j, 2048, 16), V("s9", 0, 9), True, True, last=j == 15)
-        ts(V("o1"), P(4), 8191 * MAG + 3 * PITCH + 128, None, A.add)
-        for c in range(3):
-            act(V("mb", 128 * c, 128 * c + 128), P(6), F.Relu, bias=8.0 * (c + 2), scale=-8.0)
-        if FUSE:
-            if t > 0: act(V("zsp", 0, 2048, 16), P(3), F.Abs)
-            else:
-                ms(V("zsp"), 0.0); act(V("zsp", 0, 2048, 16), V(zc), F.Copy)
-        act(V(d0n), P(7, 0, 144), F.Copy)
-        send(hop, hin if direct else "rl_%d" % t, V(d0n, 0, 128), ("ah%d" if direct else "ar%d") % t, m1)
-        if t > 0:
-            cp(V("ui"), P(5, 0, 8))
-            ts(V("zh"), P(5, 128, 256), 0.5, -0.25, A.mult, A.add)
-            ts(V("um"), V("ui"), 31, None, A.bitwise_and)
-            tt(V("uf"), V("um"), V("c32"), A.add)
-            cp(V("oc"), V("uf"))
+            group(P(3), [(V("Ib"), Y), (V("nIb"), Z)], last=False)
+            group(P(3, 128, 256), [(Y, V("Ib")), (Z, V("nIb"))], last=False)
+            group(P(3, 256, 384), [(Y, V("GGb"))])
+            group(P(2, 128, 256), [(V("Ib"), Y), (V("Ib"), Z)])
+            group(P(5), [(I(2048), V("c24")), (Y, V("GGb"))], stop=False)
         else:
-            fill(4); fill(5)
+            group(P(3, 128, 256), [(V("za"), V("Ib"))]); fill(3)
+        ts(V("o1"), P(4), 512.0, 8191 * MAG + 3 * PITCH + 512 * 2048, A.mult, A.add)
+        for c in range(3):
+            act(mk[c], P(6), F.Relu, bias=-8.0 * (c + 1), scale=8.0)
         for j in range(16):
-            mm(P(0, j, 384, 16), V("G0", j, 2048, 16), V("s24"), True, True, last=j == 15)
-        gat("act", "G1", 0, W1, "o1", 0, G1S)
-        if FUSE:
-            for n, (a, b) in enumerate(regions(GX)):
-                if n != 1: scan(V("zr", a, b), V("m16", 0, b - a), V("zsp", a, b), 0.0, A.mult, A.add)
+            mm(P(7, j, 512, 16), V("G0", j, 2048, 16), V("s32"), True, True, last=j == 15)
+        act(V(d0n, 0, 16), P(7, 112, 128), F.Copy)
+        act(d0, P(7), F.Copy)
+        send(hop, hin if direct else "rl_%d" % t, V(d0n, 0, 128), ("ah%d" if direct else "ar%d") % t, m1)
+        for c0, m in ((0, mk[0]), (128, mk[1]), (256, V("mk", 352, 384)), (288, mk[2])):
+            mm(P(1, c0, c0 + m[3] - m[2]), I(-1), m, c0 == 0, False)
         gat("dve", "G1", 0, W1, "o1", G1S, 2048)
-        for j in range(16):
-            mm(P(1, j, 384, 16), V("G1", j, 2048, 16), V("s24"), True, True, last=j == 15)
         if t > 0:
-            act(V(zn), P(3), F.Abs)
-            zc, zn = zn, zc
-        tt(V("ta"), P(0, 0, 384), V("mm"), A.min)
-        group(P(3), [(V(zc), V("nIb"))])
-        act(V("nzT"), P(3), F.Copy)
-        if t == 0: fill(8)
-        group(P(6), [(d0, I(512)), (ta[2], I(1)), mid[0], mid[2]], stop=False)
-        tt(tb[2], P(1, 256, 384), V("mb", 256, 384), A.min)
-        group(P(2, 32, 160), [(I(1), ta[2]), (I(1), tb[2])], last=False)
-        group(P(2, 0, 32), [(I(1), V("ta", 352, 384)), (I(1), V("tb", 352, 384))])
-        tt(V("tb", 0, 256), P(1, 0, 256), V("mb", 0, 256), A.min)
-        act(V(d3n), P(2, 0, 160), F.Copy)
-        send(nx2, lwn, V(d3n, 0, 128), "al%d" % t, m2)
-        group(P(6), [(tb[2], I(1)), mid[1], mid[3]], start=False)
-        group(P(5), mid, stop=False)
-        group(P(7), [(kc, I(1))], stop=False)
-        zero(P(4))
+            act(V("hA"), P(3, 256, 384), F.Identity, bias=M32 - 15.5)
+            act(Z, P(3), F.Abs)
+            group(P(5), [(I(-1), V("hA"))], start=False)
+        gat("act", "G1", 0, W1, "o1", 0, G1S)
+        act(V("zT"), P(3, 128, 256), F.Abs)
+        tt(V("ta", 0, 256), P(7, 128, 384), V("mk", 0, 256), A.min)
+        tt(V("ta", 288, 416), P(7, 384, 512), mk[2], A.min)
+        if t > 0:
+            tt(V("CS"), P(5), V("qm"), A.mult)
+            cp(V("ta", 256, 288), V("ta", 384, 416))
+            group(P(5, 128, 136), [(V("CS"), V("sel")), (I(1), V("c32h"))])
+            ts(V("zh"), P(2, 128, 256), 0.5, -0.25, A.mult, A.add)
+            cp(V("oc"), P(5, 128, 136))
+        else:
+            cp(V("ta", 256, 288), V("ta", 384, 416))
+            fill(4)
+        for j in range(16):
+            mm(P(1, j, 416, 16), V("G1", j, 2048, 16), V("s26", 0, 26), False, j == 15)
+        scan(V("zr", 0, 16 * ND), V("m16", 0, 16 * ND), V("zsp", 0, 16 * ND), 0.0, A.mult, A.add)
         if t > 0:
             emit("dve", lambda: g.vector.tensor_copy(T.X[:].indirect(T.oc[:]), T.zh[:]), [V("oc"), V("zh")], [V("X")])
-        else:
-            fill(6)
+        tt(V(dgn, 256, 416), P(1, 256, 416), V("ta", 256, 416), A.max)
+        send(nx2, lwn, V(dgn, 256, 384), "al%d" % t, m2)
+        tt(V(dgn, 0, 256), P(1, 0, 256), V("ta", 0, 256), A.max)
+        mid = [(d1, I(64)), (d2, I(8))]
+        group(P(6), [(d0, I(512)), (d3, I(1))] + mid)
+        group(P(5), mid, stop=False)
+        group(P(7), [(kc, I(1))], stop=False)
+        group(P(4), [(I(1), V("zer"))], stop=False)
+        if t == 0: fill(5)
         cp(V("oP"), P(6))
-        if t == 0: fill(7)
-        gathers(V("X"), "oP", "yy", 0, GY, None, A.subtract if FUSE else None)
         if t < RO - 1:
-            mm(P(6, 128, 256), ta[0], I(1), True, False); mm(P(6, 128, 256), tb[0], I(1), False, False)
-            group(P(6, 256, 384), [(ta[1], I(1)), (tb[1], I(1))], start=False, stop=False)
-            mm(P(6, 0, 128), d0, I(1), False, False); mm(P(6, 384, 512), d3, I(1), False, False)
+            for n, d in enumerate((d0, d1, d2, d3)): mm(P(2, 128 * n, 128 * n + 128), d, I(1), n == 0, False)
         else:
-            group(P(6), mid + [(d0, I(512)), (d3, I(1))], stop=False)
+            group(P(2), mid + [(d0, I(512)), (d3, I(1))], stop=False)
+        zdist(0, "oP", "aby")
+        mm(P(5), V(lwn), I(1), False, False, after=[("al%d" % t, n_lo)])
+        mm(P(5), V(hin), I(512), False, True, after=[("ah%d" % t, n_hi)])
+        cp(V("oM"), P(5))
+        sums(4, "yy", 0, V("grp"), ND)
 
-        def name_m():
-            mm(P(5), V(lwn), I(1), False, False, after=[("al%d" % t, n_lo)])
-            mm(P(5), V(hin), I(512), False, True, after=[("ah%d" % t, n_hi)])
-            cp(V("oM"), P(5))
-        sizes("yy", 0, "aby", True, GY, None, None, {5: name_m})
-        gathers(V("X"), "oM", "yy", 2048, GM, None, A.subtract if FUSE else None)
-
-        def diffs():
-            group(P(5), [(I(1), V(hin)), (I(-1), d0)], last=False)
-            group(P(5, 128, 256), [(I(1), V(lwn)), (I(-1), d3)])
-        sizes("yy", 2048, "ab2", True, GM, 4, V("grp"), {2: lambda: sums(4, "aby", V("ngrp"), 0, 128), 4: diffs})
-        ts(V("took"), P(4), 0.0, None, A.is_lt)
-        group(P(7), [(V("took"), I(2048))], start=False)
+        zdist(2048, "oM", "ab2", lambda: sums(4, "aby", 0, V("ngrp")))
+        sums(4, "yy", 2048, V("ngrp"), ND)
+        sums(4, "ab2", 0, V("grp"), 128, True)
+        if t == 0: fill(6); fill(7)
+        mm(P(3), I(1), V(hin), True, False); mm(P(3), I(-1), d0, False, False)
+        mm(P(3, 128, 256), I(1), V(lwn), False, False); mm(P(3, 128, 256), I(-1), d3, False, False)
+        ts(took, P(4), 0.0, None, A.is_lt)
+        group(P(7), [(took, I(2048))], start=False)
+        mm(P(3), I(64), took, False, False); mm(P(3, 128, 256), I(64), took, False, True)
+        if t == 0: fill(8)
         cp(V("ox"), P(7))
-
-        def taken():
-            tt(tk0, P(5), V("took"), A.mult)
-            tt(tk3, P(5, 128, 256), V("took"), A.mult)
+        act(V("rl"), P(3, 0, 256), F.Relu, bias=-48.0)
+        r0, r3 = V("rl", 0, 128), V("rl", 128, 256)
         if t < RO - 1:
-            for j in range(16):
-                mm(P(7, 256, 257, 1, 0, 8), V("took", j, 128, 16), V("onh", 0, 1), j == 0, j == 15)
-            col = lambda n: V(n, 0, 1, 1, 0, 8)
-
-            def count0():
-                cp(col("ai"), P(7, 256, 257, 1, 0, 8)); taken(); ts(col("am"), col("ai"), 31, None, A.bitwise_and)
-            gathers(V("yy"), "ox", "xb", 16, GX, {0: count0, 2: lambda: cp(col("af"), col("am")), 3: lambda: ts(
-                V("aE", 0, 128, 1, 0, 8), V("Egf", 0, 128, 1, 0, 8), col("af"), -1.0 / 16, A.mult, A.mult)},
-                A.add if FUSE else None)
+            group(P(5), [(took, V("onh"))])
 
             def names():
-                mm(P(6, 0, 128), tk0, I(1), False, False); mm(P(6, 384, 512), tk3, I(1), False, True)
-                if EV == 0:
-                    act(V("src", 0, 512), P(6, 0, 512), F.Copy); table(t + 1)
-            blockscan(0, 512); blockscan(512, 1024)
-            xsizes(t + 1, names)
-            if EV == 1:
-                act(V("src", 0, 512), P(6, 0, 512), F.Copy); table(t + 1)
+                group(P(2, 0, 128), [(r0, I(1)), (took, I(-16))], start=False, stop=False)
+                group(P(2, 384, 512), [(r3, I(1)), (took, I(-16))], start=False)
+                act(V("CS"), P(5), F.Copy)
+
+            def count():
+                group(P(6), [(V("CS"), V("GG"))])
+                act(V("hA"), P(6), F.Identity, bias=M32 - 15.5)
+                group(P(4), [(V("CS"), V("nGG"))], start=False, stop=False)
+            xdiffs(t + 1, V("yy"), A.add, names, count)
+            act(V("src", 0, 512), P(2, 0, 512), F.Copy); table(t + 1)
+            group(P(4), [(I(1), V("hA"))], start=False, stop=False)
+            xsums()
         else:
             def xq(a, b, e, q):
-                gat(e, "xb", 16, V("yy"), "ox", a, b)
+                gat(e, "xb", 16, V("yy"), "ox", a, b, A.add if e == "dve" else None)
                 dma("sp", "oxy%d" % q, T.xy[:, a:b], T.xb[:, 16 + a:16 + b], [V("xb", 16 + a, 16 + b)], [])
-            taken()
-            group(P(6), [(tk0, I(512)), (tk3, I(1))], start=False)
-            if FUSE:
-                gathers(V("yy"), "ox", "xb", 16, GX, None, A.add)
-                act(V("lo"), P(6), F.Copy)
-                dma("sp", "oly", T.ly[:], T.lo[:], [V("lo")], [])
-                for q, (a, b) in enumerate(((0, 768), (768, 1280), (1280, 1792), (1792, 2048))):
-                    dma("sp", "oxy%d" % q, T.xy[:, a:b], T.xb[:, 16 + a:16 + b], [V("xb", 16 + a, 16 + b)], [])
-                for q in range(4): blockscan(512 * q, 512 * q + 512)
-            else:
-                xq(0, 640, "act", 0); xq(640, 1152, "dve", 1)
-                act(V("lo"), P(6), F.Copy)
-                dma("sp", "oly", T.ly[:], T.lo[:], [V("lo")], [])
-                xq(1152, 1664, "act", 2); xq(1664, 2048, "act", 3)
-                blockscan(0, 512); blockscan(512, 1024); blockscan(1024, 1152); blockscan(1152, 1664); blockscan(1664, 2048)
-            group(P(3), [(V("Ib"), Y), (V("nIb"), V(zc))])
-            act(V(zn), P(3), F.Abs)
-            dma("act", "ozy", T.zy[:], T[zn][:], [V(zn)], [])
+            group(P(2), [(r0, I(512)), (r3, I(1)), (took, I(-8208))], start=False)
+            h = halves(NL); m = 16 * (NL // 2)
+            xq(0, m, "dve", 0); xq(h[0][0], h[0][1], "act", 1)
+            act(V("lo"), P(2), F.Copy)
+            dma("act", "oly", T.ly[:], T.lo[:], [V("lo")], [])
+            xq(m, 16 * NL, "dve", 2); xq(h[1][0], h[1][1], "act", 3)
+            blockscan(0, 16 * NL); blockscan(16 * NL, 2048)
+            group(P(3), [(V("Ib"), Y), (V("nIb"), Z)])
+            act(V("zo"), P(3), F.Abs)
+            dma("act", "ozy", T.zy[:], T.zo[:], [V("zo")], [])
     for s in ["pe", "dve", "act", "pool"] + DSEMS:
         if cnt.get(s, 0): g.wait_ge(T.sem[s], cnt[s])
     g.wait_ge(T.sem.sent, sent[0])

@@ -11,34 +11,40 @@ M32 = 49152.0
 ND = 72
 NX = 80
 NL = 72
-G0S, G1S = 960, 832
+G0S, G1S = 1120, 1120
+G1A = 576
+YB = 384
+RY = 8
+G0A = 512
+MW = 896
 F0, F1, F2 = 3072, 6656, 9728
 
 bf, f16, f32, i32, u16 = "bfloat16", "float16", "float32", "int32", "uint16"
 SB = {
     "X": (4096, bf), "tab": (TABW, bf), "xb": (2064, bf), "yy": (4096, bf), "aby": (2048, bf), "ab2": (2048, bf),
     "mx": (2048, bf), "G0": (2048, bf), "G1": (2048, bf), "ysc": (2048, bf), "nE": (2048 - 16 * ND, bf), "zr": (2048, bf),
-    "zsp": (2048, bf), "m16": (1280, bf), "m8": (1024, bf),
+    "zsp": (2048, bf), "m16": (MW, bf), "m8": (1024, bf),
     "li": (128, i32), "dgi": (512, i32), "src": (528, bf), "thi": (4, i32), "thf": (4, f32),
     "za": (128, bf), "zT": (128, bf), "zh": (128, i32), "zo": (128, bf),
     "ox": (128, u16), "o0": (128, u16), "o1": (128, u16), "oP": (128, u16), "oM": (128, u16), "oc": (8, u16),
     "uf": (8, f32), "c32": (8, i32),
     "thE": (384, f32), "Egf": (128, f32), "onf": (128, f32),
     "vb": (128, bf), "stg": (128, f32), "st2": (128, f32), "st3": (128, f32), "gi": (8, i32), "gj": (8, i32),
-    "Ib": (128, bf), "nIb": (128, bf), "ngrp": (8, bf), "grp2": (8, bf), "s32": (32, bf),
+    "Ib": (128, bf), "nIb": (128, bf), "ngrp": (8, bf), "grp2": (8, bf), "s33": (16, bf),
     "s26": (32, bf), "c16": (128, bf), "c24": (128, f16), "jF": (128, bf), "jB": (128, bf),
     "ZB": (160, bf), "ZF": (264, f32), "ZH": (416, f16), "OB": (256, bf),
     "GGb": (128, bf), "qm": (128, f16), "sel": (8, f16), "c32h": (8, f16),
     "kc": (128, f16), "dlt": (128, f16), "Eg": (128, f16), "onh": (128, f16), "GG": (128, f16), "nGG": (128, f16),
     "il": (128, bf), "jl": (128, bf), "wl": (128, bf),
     "ii": (128, f16), "jj": (128, f16), "cc": (384, f16), "cv": (384, f16), "h0": (128, f16), "h1": (128, f16),
-    "dv": (128, f16), "mk": (384, f16), "ta": (416, f16), "took": (128, f16), "rl": (256, f16), "CS": (128, f16),
+    "dv": (128, f16), "mk": (416, f16), "ta": (416, f16), "took": (128, f16), "rl": (256, f16), "CS": (128, f16),
     "hA": (128, f16), "lo": (128, f32),
 }
 PART = {"nb": ("ZB", 0, 144), "g9": ("ZB", 144, 9), "grp": ("ZB", 145, 8), "Tt": ("ZF", 0, 128), "Ssh": ("ZF", 128, 136),
         "Ibuf": ("ZH", 0, 144), "Wbuf": ("ZH", 144, 144), "zer": ("ZH", 288, 128), "onF": ("OB", 0, 128), "onB": ("OB", 128, 128)}
+MK = (0, 128, 288)
 R512 = 1.0 / 512
-SCALES = [1, 3, -1, -3, 2048, -16, 2, R512, 512, 64, 8, -8208]
+SCALES = [1, 2048, 3, -1, -3, 2, -16, R512, 512, 64, 8, -8208]
 
 
 def iname(s):
@@ -53,7 +59,7 @@ for _t in range(RO):
 SCRATCH = {k: ("sbuf", [128, w], d) for k, (w, d) in SB.items()}
 for _b in range(8):
     SCRATCH["P%d" % _b] = ("psum", [128, 512], f32)
-DSEMS = ["dl0", "dth", "dz", "dx0", "dx1", "dfl", "dfe", "oly", "ozy"] + ["oxy%d" % q for q in range(4)] \
+DSEMS = ["dl0", "dth", "dz", "dx0", "dx1", "dfl", "oly", "ozy"] + ["oxy%d" % q for q in range(4)] \
     + ["tm%d" % t for t in range(RO)] + ["ts%d" % t for t in range(RO)]
 SEMAPHORES = ["pe", "dve", "act", "pool", "sent"] + DSEMS \
     + ["ah%d" % t for t in range(RO)] + ["al%d" % t for t in range(RO)] + ["ar%d" % t for t in range(RO)]
@@ -76,7 +82,7 @@ def rank_program(g, core, T, topo):
         for r in range(N):
             src, dst = cores[r], cores[(r + 1) % N]
             if not topo.may_write(src, dst) and relay_of(src, dst, topo) == core:
-                m_in = topo.mask(src, core) & topo.mask(src, cores[(r + 2) % N]); m = topo.mask(core, dst)
+                m_in = topo.mask(src, core); m = topo.mask(core, dst)
                 rid, pid = topo.addr(dst, core)
                 for t in range(RO):
                     g.wait_ge(T.sem["ar%d" % t], nbits(m_in))
@@ -193,8 +199,8 @@ def rank_program(g, core, T, topo):
     m2 = topo.mask(core, nx2)
     direct = topo.may_write(core, nxt)
     hop = nxt if direct else relay_of(core, nxt, topo)
-    m1 = topo.mask(core, hop) & m2
-    n_hi = nbits(topo.mask(prv, core) & topo.mask(prv, nxt)) if topo.may_write(prv, core) \
+    m1 = topo.mask(core, hop)
+    n_hi = nbits(topo.mask(prv, core)) if topo.may_write(prv, core) \
         else nbits(topo.mask(relay_of(prv, core, topo), core))
     n_lo = nbits(topo.mask(cores[(rank - 2) % N], core))
     sent = [0]
@@ -219,52 +225,59 @@ def rank_program(g, core, T, topo):
             dma("sp", tsp[0], T.tab[c::16, S0:TABW], T.src[:, 128 * c:128 * c + 128], R, [V("tab", S0, TABW)], tsp)
 
     def halves(nb):
-        a = 16 * nb; m = a + (128 - nb) // 2 * 16
+        a = 16 * nb; m = a + (128 - nb) // 4 * 32
         return [(a, m), (m, 2048)]
 
-    def sums(bank, buf, c0, sel, p1=128, stop=False, p0=0):
-        for j in range(16):
+    def sums(bank, buf, c0, sel, p1=128, stop=False, p0=0, js=range(16)):
+        for j in js:
             mm(P(bank, j, 128, 16, p0, p1), V(buf, c0 + 16 * p0 + j, c0 + 16 * p1, 16), sel, False, stop and j == 15)
 
-    def zdist(c0, off, ab, pre=None):
-        hs = halves(ND)
-        gat("dve", "yy", c0, V("X"), off, 0, 16 * ND, A.subtract)
+    def zdist(c0, off, ab, pre=None, mid=None):
+        hs = halves(ND); vs = [(0, 16 * ND - YB), (16 * ND - YB, 16 * ND)]
+        for a, b in vs: gat("dve", "yy", c0, V("X"), off, a, b, A.subtract)
         for a, b in hs: gat("act", "yy", c0, V("X"), off, a, b)
-        ts(V(ab, 0, 16 * ND), V("yy", c0, c0 + 16 * ND), 0.0, 2.0, A.max, A.mult)
-        if pre: pre()
         for n, (a, b) in enumerate(hs):
+            if pre: pre(n)
             group(P(n, 0, b - a), [(V("zT"), V("nE", a - 16 * ND, b - 16 * ND)), (V("Ib"), V("yy", c0 + a, c0 + b))])
             act(V(ab, a, b), P(n, 0, b - a), F.Abs)
+        for n, (a, b) in enumerate(vs):
+            ts(V(ab, a, b), V("yy", c0 + a, c0 + b), 0.0, 2.0, A.max, A.mult)
+            if n == 0 and mid: mid()
 
     def xdiffs(t, win, op, mid=None, mid2=None):
-        hs = halves(NX)[::-1]
-        gat("dve", "xb", 16, win, "ox", 0, 16 * NX, op)
-        for a, b in hs: gat("act", "xb", 16, win, "ox", a, b)
-        scan(V("mx", 0, 16 * NX), V("xb", 15, 15 + 16 * NX), V("xb", 16, 16 + 16 * NX), 1024.0, A.min, A.max)
+        hs = halves(NX)
+        gat("dve", "xb", 16, win, "ox", 16 * (NX - 16), 16 * NX, op)
+        gat("dve", "xb", 16, win, "ox", 0, 16 * (NX - 16), op)
         mm(P(4), V("onf", 0, 128, 1, 0, 8), V("thE", 128 * t, 128 * t + 128, 1, 0, 8), True, False)
-        if mid: mid()
         for n, (a, b) in enumerate(hs):
+            gat("act", "xb", 16, win, "ox", a, b)
+            if n == 0 and mid: mid()
             group(P(n, 0, b - a), [(V("Ib"), V("xb", 16 + a, 16 + b)), (V("nIb"), V("xb", 15 + a, 15 + b))])
+            if n == 0 and mid2: mid2(0)
+        scan(V("mx", 0, 16 * NX), V("xb", 15, 15 + 16 * NX), V("xb", 16, 16 + 16 * NX), 1024.0, A.min, A.max)
+        for n, (a, b) in enumerate(hs):
             act(V("mx", a, b), P(n, 0, b - a), F.Abs, scale=0.5)
-            if n == 0 and mid2: mid2()
+            if mid2: mid2(n + 1)
         for j in range(16):
             mm(P(7, j, 128, 16, 0, NX), V("xb", 16 + j, 16 + 16 * NX, 16), V("g9", 1, 9), True, True, last=j == 15)
-        cp(V("Ssh", 1, 129, 1, 0, NX), P(7, 0, 128, 1, 0, NX))
+        act(V("Ssh", 1, 129, 1, 0, NX), P(7, 0, 128, 1, 0, NX), F.Copy)
+        if t > 0:
+            blockscan(16 * NX, 2048)
+            scan(V("ysc", 1, 16 * NX, 2), V("m8", 0, 8 * NX), V("mx", 1, 16 * NX, 2), 0.0, A.min, A.max)
         tt(V("Tt", 0, 128, 1, 0, NX), P(7, 0, 128, 1, 0, NX), V("Ssh", 0, 128, 1, 0, NX), A.add)
         mm(P(4, 0, 128, 16, 0, NX), V("xb", 31, 16 + 16 * NX, 16), V("g9", 0, 8), False, False)
         mm(P(4, 0, 128, 16, 0, NX), V("xb", 15, 15 + 16 * NX, 16), V("ngrp"), False, False)
 
     def xsums(): sums(4, "mx", 0, V("grp2"), 128, True)
 
-    def blockmax(n):
-        if n == 0: scan(V("ysc", 1, 16 * NX, 2), V("m8", 0, 8 * NX), V("mx", 1, 16 * NX, 2), 0.0, A.mult, A.max)
-        else: blockscan(*halves(NX)[n - 1])
-
     def blockscan(a, b):
-        scan(V("ysc", a, b), V("m16", 0, b - a), V("xb", 16 + a, 16 + b), 0.0, A.mult, A.max)
+        scan(V("ysc", a, b), V("m16", 0, b - a), V("xb", 16 + a, 16 + b), 0.0, A.min, A.max)
+
+    def spread(a, b):
+        scan(V("zr", a, b), V("m16", 0, b - a), V("zsp", a, b), 0.0, A.min, A.max)
 
     dma("sp", "dl0", T.li[:], T.l0[:], [], [V("li")])
-    dma("sp", "dth", T.thi[0:8, 0:3], T.th[:], [], [V("thi")])
+    dma("act", "dth", T.thi[0:8, 0:3], T.th[:], [], [V("thi")])
     dma("sp", "dx0", T.X[:, 0:2048], T.x0[:, 0:2048], [], [V("X", 0, 2048)])
     dma("act", "dx1", T.X[:, 2048:4096], T.x0[:, 2048:4096], [], [V("X", 2048, 4096)])
     dma("sp", "dz", T.za[:], T.z0[:], [], [V("za")])
@@ -281,7 +294,10 @@ def rank_program(g, core, T, topo):
     iota(V("c32"), [[512, 8]], 0, 32)
     ms(V("tab", 1024, F0), 0.0)
     dma("sp", "dfl", T.tab[:, F1:F2], T.tab[:, 0:F2 - F1], [V("tab", 0, F2 - F1), V("X")], [V("tab", F1, F2)])
-    dma("sp", "dfe", T.nE[:], T.tab[:, 0:2048 - 16 * ND], [V("tab", 0, 2048 - 16 * ND), V("X")], [V("nE")])
+    iota(V("zsp", 0, 16 * ND), [[0, 16 * ND]], 0, 0)
+    emit("pool", lambda: g.affine_select(T.nE[:], T.zsp[:, 0:2048 - 16 * ND], [[1, 128 - ND], [0, 16]], A.not_equal, -1.0, ND, -1),
+         [V("zsp", 0, 2048 - 16 * ND)], [V("nE")])
+    iota(V("m16"), [[0, MW // 16], [256, 16]], 0, 0)
     ts(V("Ib"), V("vb"), 0.0, None, A.is_equal)
     ts(V("nIb"), V("vb"), 0.0, -1.0, A.is_equal, A.mult)
     ts(V("gj"), V("gi"), 4, None, A.arith_shift_right)
@@ -295,177 +311,168 @@ def rank_program(g, core, T, topo):
     def threshold(t):
         ts(V("thE", 128 * t, 128 * t + 128, 1, 0, 8), V("Egf", 0, 128, 1, 0, 8), V("thf", t, t + 1, 1, 0, 8), -1.0, A.mult, A.mult)
     threshold(0)
-    ms(V("src", 512, 528), 0.0); ms(V("OB"), 1.0); ms(V("c16"), 16.0); ms(V("onh"), 1.0)
-    ms(V("onF", 0, 128, 16), BIG); ms(V("onB", 15, 128, 16), BIG)
+    ms(V("src", 512, 528), 0.0); ms(V("OB"), 1.0)
+    for p in range(4):
+        ts(V("dgi", 128 * p, 128 * p + 128), V("li"), 3 * (3 - p), 7, A.logical_shift_right, A.bitwise_and)
 
-    def digits():
-        for p in range(4):
-            ts(V("dgi", 128 * p, 128 * p + 128), V("li"), 3 * (3 - p), 7, A.logical_shift_right, A.bitwise_and)
-    xdiffs(0, V("X"), None, digits)
-    cp(V("src", 0, 512), V("dgi"))
-    table(0)
-    emit("pool", lambda: g.affine_select(T.nE[:], T.nE[:], [[1, 128 - ND], [0, 16]], A.not_equal, -1.0, ND, -1), [V("nE")], [V("nE")])
+    def digits(n):
+        if n == 1:
+            cp(V("src", 0, 512), V("dgi")); table(0)
+        if n == 2:
+            act(V("onF", 0, 128, 16), V("onf", 0, 8), F.Copy, scale=BIG)
+            act(V("onB", 15, 128, 16), V("onf", 0, 8), F.Copy, scale=BIG)
+            act(V("c16"), V("onf"), F.Copy, scale=16.0); act(V("onh"), V("onf"), F.Copy)
+            act(I(2048), V("Ib"), F.Copy, scale=2048.0)
+    xdiffs(0, V("X"), None, None, digits)
     act(V("Eg"), V("Egf"), F.Copy)
     xsums()
-    group(P(3), [(V("Eg", 0, 128, 1, 0, 8), V("Eg", 0, 128, 1, 0, 8))])
-    act(V("kc"), V("st2"), F.Copy)
+    group(P(3), [(V("Eg", 0, 128, 1, 0, 8), V("Eg", 0, 128, 1, 0, 8))], last=False)
+    group(P(3, 128, 256), [(V("za"), V("Ib"))])
+    act(I(1), V("Ib"), F.Copy)
     act(V("dlt"), V("st3"), F.Copy, scale=1.0 / 1024)
     act(V("dlt", 0, 128, 16), V("onf", 0, 8), F.Copy, scale=385.0 / 1024)
-    act(I(1), V("Ib"), F.Copy)
+    act(V("kc"), V("st2"), F.Copy)
+    for s in SCALES[2:11]: act(I(s), V("Ib"), F.Copy, scale=float(s))
     act(V("GG"), P(3), F.Copy); act(V("nGG"), P(3), F.Copy, scale=-1.0); act(V("GGb"), P(3), F.Copy)
-    for s in SCALES[1:8]: act(I(s), V("Ib"), F.Copy, scale=float(s))
 
     def fill(n):
         if n == 0:
-            ms(V("m16", 0, 768), 1.0)
+            cp(V("s33", 0, 1), V("Ib", 112, 113)); cp(V("s33", 1, 9), V("Ib", 0, 128, 16))
+            cp(V("s26", 0, 8), V("Ib", 1, 128, 16))
         if n == 1:
-            ms(V("m16", 768, 1280), 1.0); ms(V("m16", 0, 1280, 16), 0.0)
-            for c in range(4): act(V("s32", 8 * c, 8 * c + 8), V("Ib", c, 128, 16), F.Copy)
+            cp(V("s26", 8, 16), V("Ib", 2, 128, 16)); cp(V("s26", 16, 18), V("Ib", 99, 128, 16)); cp(V("s26", 18, 26), V("Ib", 3, 128, 16))
         if n == 2:
-            ms(V("zsp", 0, 576), 0.0)
-        if n == 3:
-            act(V("s26", 0, 16), V("s32", 8, 24), F.Copy)
-            act(V("s26", 18, 26), V("s32", 24, 32), F.Copy)
-            act(V("s26", 16, 18), V("s32", 30, 32), F.Copy)
-        if n == 4:
-            ms(V("zsp", 576, 16 * ND), 0.0); cp(V("zsp", 0, 2048, 16), V("za"))
-            for s in SCALES[8:11]: ts(I(s), V("vb"), 0.0, float(s), A.is_equal, A.mult)
-        if n == 5:
             ms(V("zr", 16 * ND, 16 * max(NX, NL, ND + 1)), 0.0)
+        if n == 5:
             ts(V("gj"), V("c32"), 9, None, A.arith_shift_right)
             ts(V("thf", 1, 3, 1, 0, 8), V("thf", 1, 3, 1, 0, 8), M32, None, A.add)
         if n == 6:
             threshold(1); cp(V("sel"), V("grp"))
             ts(V("uf", 0, 1), V("gj", 0, 1), 512.0, None, A.mult)
-        if n == 7:
-            ms(V("m8", 0, 8 * NX), 1.0); ms(V("c24"), M32 / 2048)
+            ms(V("c24"), M32 / 2048)
             ts(V("c32h"), V("c32"), V("uf", 0, 1), None, A.subtract)
-            ms(V("m8", 0, 8 * NX, 8), 0.0)
             ts(V("uf", 1, 2), V("c32h", 0, 1), 1.0 / 32, V("st2", 0, 1), A.mult, A.add)
-        if n == 8:
+        if n == 7:
             ts(V("qm"), V("st2"), V("uf", 1, 2), None, A.is_equal)
+        if n == 8:
             threshold(2); ts(I(-8208), V("vb"), 0.0, -8208.0, A.is_equal, A.mult)
 
     Y, Z = V("ysc", 15, 2048, 16), V("zsp", 0, 2048, 16)
     ii, jj, kc, took = V("ii"), V("jj"), V("kc"), V("took")
     cs = [V("cc", 128 * n, 128 * n + 128) for n in range(3)]
     cv = [V("cv", 128 * n, 128 * n + 128) for n in range(3)]
-    mk = [V("mk", 128 * n, 128 * n + 128) for n in range(3)]
     for t in range(RO):
         d0n, dgn, hin, lwn = "d0_%d" % t, "dg_%d" % t, "hi_%d" % t, "lw_%d" % t
         d0, d1, d2, d3 = V(d0n, 16, 144), V(dgn, 0, 128), V(dgn, 128, 256), V(dgn, 288, 416)
 
-        def gap(n):
-            if t == 0: fill(n)
-            elif n < 3: blockmax(n)
+        if t > 0:
+            group(P(3), [(V("Ib"), Y), (V("nIb"), Z)], last=False)
+            group(P(3, 256, 384), [(Y, V("GGb"))], last=False)
+            group(P(3, 128, 256), [(Y, V("Ib")), (Z, V("nIb"))], last=False)
+            group(P(3, 384, 512), [(V("Ib"), Y), (V("Ib"), Z)])
+            act(Z, P(3), F.Abs)
+            act(V("hA"), P(3, 256, 384), F.Identity, bias=M32 - 15.5)
+        act(V("zT"), P(3, 128, 256), F.Abs)
         tt(V("nb", 0, 128), P(4), V("Tt"), A.is_le)
         scan(V("il"), V("onF"), V("nb", 0, 128), 0.0, A.add, A.mult)
         scan(V("wl", 0, 128, -1), V("onB", 0, 128, -1), V("nb", 0, 128, -1), 0.0, A.add, A.mult)
         group(P(7, 0, 128, 1, 0, 8), [(V("il", 15, 128, 16), V("Ib"))])
         group(P(0, 0, 128, 1, 0, 8), [(V("wl", 0, 128, 16), V("Ib"))])
         scan(V("jl", 0, 128, -1), V("nb", 1, 129, -1), V("onB", 0, 128, -1), 0.0, A.mult, A.add)
-        group(P(3), [(I(1), V("dlt"))], stop=False)
-        group(P(4), [(kc, I(1))], stop=False)
-        group(P(5), [(V("Ib"), V("jF"))], stop=False)
-        group(P(6), [(V("Ib"), V("jB"))], stop=False)
+        group(P(5), [(V("Ib"), V("jF"))], stop=False); group(P(6), [(V("Ib"), V("jB"))], stop=False)
+        mm(P(1), I(2048), V("onh"), True, False)
         scan(V("Ibuf", 1, 129, 1, 0, 8), V("c16", 0, 128, 1, 0, 8), P(7, 0, 128, 1, 0, 8), 0.0, A.add, A.min)
         scan(V("Wbuf", 0, 128, -1, 0, 8), V("c16", 0, 128, 1, 0, 8), P(0, 0, 128, -1, 0, 8), 0.0, A.add, A.min)
         group(P(5), [(V("Ibuf", 0, 128, 1, 0, 8), V("Eg", 0, 128, 1, 0, 8))], start=False)
-        group(P(7), [(kc, I(1))], stop=False)
+        group(P(4, 128, 256), [(I(1), V("dlt"))], stop=False)
         group(P(6), [(V("Wbuf", 1, 129, 1, 0, 8), V("Eg", 0, 128, 1, 0, 8))], start=False)
         group(P(2), [(I(1), kc)], stop=False)
-        for n in range(3): mm(P(1, 128 * n, 128 * n + 128), I(2048), V("onh"), n == 0, False)
+        group(P(7), [(kc, I(1))], stop=False)
+        if t > 0: group(P(3, 256, 384), [(I(2048), V("c24")), (Y, V("GGb")), (I(-1), V("hA"))])
         tt(ii, P(5), V("il"), A.min)
         tt(jj, P(6), V("jl"), A.min)
-        for n, a in enumerate((3, 1, 1)): mm(P(0, 128 * n, 128 * n + 128), I(a), ii, n == 0, False)
-        for n, b in enumerate((-1, -1, -3)): mm(P(0, 128 * n, 128 * n + 128), I(b), jj, False, n == 2)
-        for n in range(3):
-            group(P(1, 128 * n, 128 * n + 128), [(I(-1), ii), (I(-1), jj)], start=False, stop=n == 2)
+        mm(P(0), I(3), ii, True, False); mm(P(5), I(1), ii, True, False); mm(P(1), I(-1), ii, False, False)
+        mm(P(0), I(-1), jj, False, True); mm(P(5), I(-1), jj, False, True)
+        group(P(6), [(I(1), ii), (I(-3), jj)])
+        mm(P(1), I(-1), jj, False, True)
+        if t > 0: spread(0, 8 * ND)
+        else: fill(0)
         group(P(2), [(I(3), ii)], start=False, stop=False)
         group(P(7), [(ii, I(3))], start=False, stop=False)
-        group(P(3), [(I(-16), ii), (I(-16), jj)], start=False)
+        group(P(4, 128, 256), [(I(-16), ii), (I(-16), jj)], start=False)
+        for n, b in enumerate((0, 5, 6)): ts(cs[n], P(b), 0.0, None, A.is_ge)
+        act(V("dv"), P(4, 128, 256), F.Relu, bias=32.0, scale=2.0)
+        group(P(0), [(I(1), jj), (I(-3), ii)], stop=False)
         group(P(5), [(I(1), kc), (I(2), ii), (I(-1), jj)], stop=False)
-        group(P(4), [(ii, I(2)), (jj, I(-1))], start=False, stop=False)
-        gap(0)
-        ts(V("cc"), P(0, 0, 384), 0.0, None, A.is_ge)
-        tt(V("cv"), P(1, 0, 384), V("cc"), A.mult)
-        act(V("dv"), P(3), F.Relu, bias=32.0, scale=2.0)
-        group(P(2), [(I(1), c) for c in cv], start=False)
+        group(P(0), [(I(2048), c) for c in cs], start=False, stop=False)
+        for n in range(3):
+            tt(cv[n], P(1), cs[n], A.mult)
+            mm(P(2), I(1), cv[n], False, n == 2)
+            mm(P(7), cv[n], I(1), False, False)
+        group(P(0), [(I(-1), c) for c in cv], start=False)
         group(P(5), [(I(1), c) for c in cv], start=False)
-        group(P(7), [(c, I(1)) for c in cv], start=False, stop=False)
-        gap(1)
+        for c in range(3):
+            act(V("mk", MK[c], MK[c] + 128), P(0), F.Relu, bias=-8.0 * (c + 1), scale=8.0)
+        if t > 0:
+            tt(V("CS"), P(3, 256, 384), V("qm"), A.mult)
+            ts(V("zh"), P(3, 384, 512), 0.5, -0.25, A.mult, A.add)
+        else: fill(1)
         ts(V("h0"), P(2), 1.0 / 16, HC, A.mult, A.add)
         group(P(7), [(V("h0"), I(-16)), (V("h0"), I(R512))], start=False)
-        act(V("h1"), P(5), F.Identity, bias=HC + 128, scale=1.0 / 16)
-        group(P(4), [(c, I(1)) for c in cv] + [(V("dv"), I(1)), (V("h1"), I(-16)), (V("h1"), I(R512))], start=False)
-        group(P(6), [(I(1), jj), (I(-3), ii)] + [(I(2048), c) for c in cs] + [(I(-1), c) for c in cv])
-        gap(2)
+        if t > 0: group(P(3, 0, 8), [(V("CS"), V("sel")), (I(1), V("c32h"))])
+        group(P(4), [(kc, I(1)), (ii, I(2)), (jj, I(-1))] + [(c, I(1)) for c in cv] + [(V("dv"), I(1))], stop=False)
+        if t > 0: spread(8 * ND, 16 * ND)
+        else: fill(2)
         ts(V("o0"), P(7), 512.0, 8191 * MAG + 3 * PITCH, A.mult, A.add)
+        ts(V("h1"), P(5), 1.0 / 16, HC + 128, A.mult, A.add)
+        group(P(4), [(V("h1"), I(-16)), (V("h1"), I(R512))], start=False)
         W0, W1 = V("tab", 0, S0), V("tab")
         gat("act", "G0", 0, W0, "o0", 0, G0S)
-        gat("dve", "G0", 0, W0, "o0", G0S, 2048)
-        if t > 0:
-            group(P(3), [(V("Ib"), Y), (V("nIb"), Z)], last=False)
-            group(P(3, 128, 256), [(Y, V("Ib")), (Z, V("nIb"))], last=False)
-            group(P(3, 256, 384), [(Y, V("GGb"))])
-            group(P(2, 128, 256), [(V("Ib"), Y), (V("Ib"), Z)])
-            group(P(5), [(I(2048), V("c24")), (Y, V("GGb"))], stop=False)
-        else:
-            group(P(3, 128, 256), [(V("za"), V("Ib"))]); fill(3)
+        gat("dve", "G0", 0, W0, "o0", G0S, G0S + G0A)
+        if t > 0: cp(V("oc"), P(3, 0, 8))
         ts(V("o1"), P(4), 512.0, 8191 * MAG + 3 * PITCH + 512 * 2048, A.mult, A.add)
-        for c in range(3):
-            act(mk[c], P(6), F.Relu, bias=-8.0 * (c + 1), scale=8.0)
+        gat("dve", "G0", 0, W0, "o0", G0S + G0A, 2048)
+        act(V("mk", 256, 288), V("mk", 384, 416), F.Copy)
         for j in range(16):
-            mm(P(7, j, 512, 16), V("G0", j, 2048, 16), V("s32"), True, True, last=j == 15)
-        act(V(d0n, 0, 16), P(7, 112, 128), F.Copy)
-        act(d0, P(7), F.Copy)
+            mm(P(7, j, 144, 16), V("G0", j, 2048, 16), V("s33", 0, 9), True, True, last=j == 15)
+        gat("dve", "G1", 0, W1, "o1", 2048 - G1A, 2048)
+        cp(V(d0n), P(7, 0, 144))
         send(hop, hin if direct else "rl_%d" % t, V(d0n, 0, 128), ("ah%d" if direct else "ar%d") % t, m1)
-        for c0, m in ((0, mk[0]), (128, mk[1]), (256, V("mk", 352, 384)), (288, mk[2])):
-            mm(P(1, c0, c0 + m[3] - m[2]), I(-1), m, c0 == 0, False)
-        gat("dve", "G1", 0, W1, "o1", G1S, 2048)
-        if t > 0:
-            act(V("hA"), P(3, 256, 384), F.Identity, bias=M32 - 15.5)
-            act(Z, P(3), F.Abs)
-            group(P(5), [(I(-1), V("hA"))], start=False)
+        for j in range(16):
+            mm(P(0, j, 416, 16), V("G0", j, 2048, 16), V("s26", 0, 26), True, True, last=j == 15)
+        mm(P(1, 0, 416), I(-1), V("mk"), True, False)
+        if t == 0: act(Z, V("za"), F.Copy)
+        gat("dve", "G1", 0, W1, "o1", G1S, 2048 - G1A)
         gat("act", "G1", 0, W1, "o1", 0, G1S)
-        act(V("zT"), P(3, 128, 256), F.Abs)
-        tt(V("ta", 0, 256), P(7, 128, 384), V("mk", 0, 256), A.min)
-        tt(V("ta", 288, 416), P(7, 384, 512), mk[2], A.min)
-        if t > 0:
-            tt(V("CS"), P(5), V("qm"), A.mult)
-            cp(V("ta", 256, 288), V("ta", 384, 416))
-            group(P(5, 128, 136), [(V("CS"), V("sel")), (I(1), V("c32h"))])
-            ts(V("zh"), P(2, 128, 256), 0.5, -0.25, A.mult, A.add)
-            cp(V("oc"), P(5, 128, 136))
-        else:
-            cp(V("ta", 256, 288), V("ta", 384, 416))
-            fill(4)
         for j in range(16):
             mm(P(1, j, 416, 16), V("G1", j, 2048, 16), V("s26", 0, 26), False, j == 15)
-        scan(V("zr", 0, 16 * ND), V("m16", 0, 16 * ND), V("zsp", 0, 16 * ND), 0.0, A.mult, A.add)
-        if t > 0:
+        tt(V("ta"), P(0, 0, 416), V("mk"), A.min)
+        if t == 0: spread(0, 8 * ND); spread(8 * ND, 16 * ND)
+        if t == 0: fill(5)
+        else:
             emit("dve", lambda: g.vector.tensor_copy(T.X[:].indirect(T.oc[:]), T.zh[:]), [V("oc"), V("zh")], [V("X")])
         tt(V(dgn, 256, 416), P(1, 256, 416), V("ta", 256, 416), A.max)
         send(nx2, lwn, V(dgn, 256, 384), "al%d" % t, m2)
+        if t == 0: iota(V("m8", 0, 8 * NX), [[0, NX], [256, 8]], 0, 0)
         tt(V(dgn, 0, 256), P(1, 0, 256), V("ta", 0, 256), A.max)
         mid = [(d1, I(64)), (d2, I(8))]
         group(P(6), [(d0, I(512)), (d3, I(1))] + mid)
         group(P(5), mid, stop=False)
         group(P(7), [(kc, I(1))], stop=False)
         group(P(4), [(I(1), V("zer"))], stop=False)
-        if t == 0: fill(5)
         cp(V("oP"), P(6))
         if t < RO - 1:
             for n, d in enumerate((d0, d1, d2, d3)): mm(P(2, 128 * n, 128 * n + 128), d, I(1), n == 0, False)
         else:
             group(P(2), mid + [(d0, I(512)), (d3, I(1))], stop=False)
-        zdist(0, "oP", "aby")
-        mm(P(5), V(lwn), I(1), False, False, after=[("al%d" % t, n_lo)])
-        mm(P(5), V(hin), I(512), False, True, after=[("ah%d" % t, n_hi)])
-        cp(V("oM"), P(5))
-        sums(4, "yy", 0, V("grp"), ND)
 
-        zdist(2048, "oM", "ab2", lambda: sums(4, "aby", 0, V("ngrp")))
+        def name_m():
+            mm(P(5), V(lwn), I(1), False, False, after=[("al%d" % t, n_lo)])
+            mm(P(5), V(hin), I(512), False, True, after=[("ah%d" % t, n_hi)])
+            cp(V("oM"), P(5))
+            sums(4, "yy", 0, V("grp"), ND)
+        zdist(0, "oP", "aby", None, name_m)
+        zdist(2048, "oM", "ab2", lambda n: sums(4, "aby", 0, V("ngrp"), js=range(RY) if n == 0 else range(RY, 16)))
         sums(4, "yy", 2048, V("ngrp"), ND)
         sums(4, "ab2", 0, V("grp"), 128, True)
         if t == 0: fill(6); fill(7)
@@ -476,9 +483,9 @@ def rank_program(g, core, T, topo):
         mm(P(3), I(64), took, False, False); mm(P(3, 128, 256), I(64), took, False, True)
         if t == 0: fill(8)
         cp(V("ox"), P(7))
-        act(V("rl"), P(3, 0, 256), F.Relu, bias=-48.0)
         r0, r3 = V("rl", 0, 128), V("rl", 128, 256)
         if t < RO - 1:
+            act(V("rl"), P(3, 0, 256), F.Relu, bias=-48.0)
             group(P(5), [(took, V("onh"))])
 
             def names():
@@ -486,10 +493,11 @@ def rank_program(g, core, T, topo):
                 group(P(2, 384, 512), [(r3, I(1)), (took, I(-16))], start=False)
                 act(V("CS"), P(5), F.Copy)
 
-            def count():
-                group(P(6), [(V("CS"), V("GG"))])
-                act(V("hA"), P(6), F.Identity, bias=M32 - 15.5)
-                group(P(4), [(V("CS"), V("nGG"))], start=False, stop=False)
+            def count(n):
+                if n == 0:
+                    group(P(6), [(V("CS"), V("GG"))])
+                    group(P(4), [(V("CS"), V("nGG"))], start=False, stop=False)
+                if n == 1: act(V("hA"), P(6), F.Identity, bias=M32 - 15.5)
             xdiffs(t + 1, V("yy"), A.add, names, count)
             act(V("src", 0, 512), P(2, 0, 512), F.Copy); table(t + 1)
             group(P(4), [(I(1), V("hA"))], start=False, stop=False)
@@ -498,13 +506,14 @@ def rank_program(g, core, T, topo):
             def xq(a, b, e, q):
                 gat(e, "xb", 16, V("yy"), "ox", a, b, A.add if e == "dve" else None)
                 dma("sp", "oxy%d" % q, T.xy[:, a:b], T.xb[:, 16 + a:16 + b], [V("xb", 16 + a, 16 + b)], [])
-            group(P(2), [(r0, I(512)), (r3, I(1)), (took, I(-8208))], start=False)
-            h = halves(NL); m = 16 * (NL // 2)
+            h = halves(NL); m = 32 * (NL // 6)
             xq(0, m, "dve", 0); xq(h[0][0], h[0][1], "act", 1)
+            xq(h[1][0], h[1][1], "act", 3); xq(m, 16 * NL, "dve", 2)
+            act(V("rl"), P(3, 0, 256), F.Relu, bias=-48.0)
+            group(P(2), [(r0, I(512)), (r3, I(1)), (took, I(-8208))], start=False)
             act(V("lo"), P(2), F.Copy)
             dma("act", "oly", T.ly[:], T.lo[:], [V("lo")], [])
-            xq(m, 16 * NL, "dve", 2); xq(h[1][0], h[1][1], "act", 3)
-            blockscan(0, 16 * NL); blockscan(16 * NL, 2048)
+            blockscan(0, m); blockscan(16 * NL, 2048); blockscan(m, 16 * NL)
             group(P(3), [(V("Ib"), Y), (V("nIb"), Z)])
             act(V("zo"), P(3), F.Abs)
             dma("act", "ozy", T.zy[:], T.zo[:], [V("zo")], [])

from concourse.mybir import AluOpType as A, ActivationFunctionType as F

RO = 3
PITCH = 512
S0 = 19 * PITCH
TABW = S0 + 2048
BIG = 4096.0
MAG = 1088.0
HC = MAG - 7.5 / 16
M32 = 49152.0
ND = 72
NX = 80
NL = 72
G0S, G1S = 1120, 1120
G1A = 576
YB = 384
RY = 8
G0A = 512
MW = 896
F0, F1, F2 = 3072, 6656, 9728

bf, f16, f32, i32, u16 = "bfloat16", "float16", "float32", "int32", "uint16"
SB = {
    "X": (4096, bf), "tab": (TABW, bf), "xb": (2064, bf), "yy": (4096, bf), "aby": (2048, bf), "ab2": (2048, bf),
    "mx": (2048, bf), "G0": (2048, bf), "G1": (2048, bf), "ysc": (2048, bf), "nE": (2048 - 16 * ND, bf), "zr": (2048, bf),
    "zsp": (2048, bf), "m16": (MW, bf), "m8": (1024, bf),
    "li": (128, i32), "dgi": (512, i32), "src": (528, bf), "thi": (4, i32), "thf": (4, f32),
    "za": (128, bf), "zT": (128, bf), "zh": (128, i32), "zo": (128, bf),
    "ox": (128, u16), "o0": (128, u16), "o1": (128, u16), "oP": (128, u16), "oM": (128, u16), "oc": (8, u16),
    "uf": (8, f32), "c32": (8, i32),
    "thE": (384, f32), "Egf": (128, f32), "onf": (128, f32),
    "vb": (128, bf), "stg": (128, f32), "st2": (128, f32), "st3": (128, f32), "gi": (8, i32), "gj": (8, i32),
    "Ib": (128, bf), "nIb": (128, bf), "ngrp": (8, bf), "grp2": (8, bf), "s33": (16, bf),
    "s26": (32, bf), "c16": (128, bf), "c24": (128, f16), "jF": (128, bf), "jB": (128, bf),
    "ZB": (160, bf), "ZF": (264, f32), "ZH": (416, f16), "OB": (256, bf),
    "GGb": (128, bf), "qm": (128, f16), "sel": (8, f16), "c32h": (8, f16),
    "kc": (128, f16), "dlt": (128, f16), "Eg": (128, f16), "onh": (128, f16), "GG": (128, f16), "nGG": (128, f16),
    "il": (128, bf), "jl": (128, bf), "wl": (128, bf),
    "ii": (128, f16), "jj": (128, f16), "cc": (384, f16), "cv": (384, f16), "h0": (128, f16), "h1": (128, f16),
    "dv": (128, f16), "mk": (416, f16), "ta": (416, f16), "took": (128, f16), "rl": (256, f16), "CS": (128, f16),
    "hA": (128, f16), "lo": (128, f32),
}
PART = {"nb": ("ZB", 0, 144), "g9": ("ZB", 144, 9), "grp": ("ZB", 145, 8), "Tt": ("ZF", 0, 128), "Ssh": ("ZF", 128, 136),
        "Ibuf": ("ZH", 0, 144), "Wbuf": ("ZH", 144, 144), "zer": ("ZH", 288, 128), "onF": ("OB", 0, 128), "onB": ("OB", 128, 128)}
MK = (0, 128, 288)
R512 = 1.0 / 512
SCALES = [1, 2048, 3, -1, -3, 2, -16, R512, 512, 64, 8, -8208]


def iname(s):
    return "Ir" if s == R512 else "I%s%d" % ("m" if s < 0 else "", abs(s))


for _s in SCALES:
    SB[iname(_s)] = (128, f16)
for _t in range(RO):
    SB["d0_%d" % _t] = (144, f16); SB["dg_%d" % _t] = (416, f16)
    SB["hi_%d" % _t] = (128, f16); SB["lw_%d" % _t] = (128, f16); SB["rl_%d" % _t] = (128, f16)
SCRATCH = {k: ("sbuf", [128, w], d) for k, (w, d) in SB.items()}
for _b in range(8):
    SCRATCH["P%d" % _b] = ("psum", [128, 512], f32)
DSEMS = ["dl0", "dth", "dz", "dx0", "dx1", "dfl", "oly", "ozy"] + ["oxy%d" % q for q in range(4)] \
    + ["tm%d" % t for t in range(RO)] + ["ts%d" % t for t in range(RO)]
SEMAPHORES = ["pe", "dve", "act", "pool", "sent"] + DSEMS \
    + ["ah%d" % t for t in range(RO)] + ["al%d" % t for t in range(RO)] + ["ar%d" % t for t in range(RO)]


def relay_of(src, dst, topo):
    c = [k for k in topo.cores_of(src) if k != src and topo.may_write(k, dst)]
    same = [k for k in c if topo.die(k) == topo.die(src)]
    return (same or c)[0]


def nbits(m):
    return bin(m).count("1")


def rank_program(g, core, T, topo):
    cores = list(T.cores); N = len(cores)
    rank = T.rank_of(core)
    if rank is None:
        for r in range(N):
            src, dst = cores[r], cores[(r + 1) % N]
            if not topo.may_write(src, dst) and relay_of(src, dst, topo) == core:
                m_in = topo.mask(src, core); m = topo.mask(core, dst)
                rid, pid = topo.addr(dst, core)
                for t in range(RO):
                    g.wait_ge(T.sem["ar%d" % t], nbits(m_in))
                    g.remote_dma(T["hi_%d" % t][:], T["rl_%d" % t][:], T.sem["ah%d" % t], T.sem.sent, pid, rid, m)
                g.wait_ge(T.sem.sent, RO * nbits(m))
        return
    Q = {"pe": g.tensor, "dve": g.vector, "act": g.scalar, "pool": g, "sp": g.sync}
    cnt = {}; known = {q: {} for q in Q}; clock = {}; hist = {}

    def psum(name): return name[0] == "P" and name[1:].isdigit()

    def V(name, c0=None, c1=None, st=1, p0=0, p1=128):
        if name in PART:
            b, o, w = PART[name]
            return V(b, o + (c0 or 0), o + (w if c0 is None else c1), st, p0, p1)
        if c0 is None: c0, c1 = 0, (512 if psum(name) else SB[name][0])
        if st == 1: ap = T[name][p0:p1, c0:c1]
        elif st > 0: ap = T[name][p0:p1, c0:c1:st]
        else: ap = T[name][p0:p1, c1 - 1:(c0 - 1 if c0 > 0 else None):-1]
        return (ap, name, c0, c1, abs(st), p0, p1)

    def meet(a, e, pad):
        if a[6] <= e[7] or e[8] <= a[5]: return False
        a0, a1 = (a[2] // 8 * 8, (a[3] + 7) // 8 * 8) if pad else (a[2], a[3])
        if not (e[0] < a1 and a0 < e[1]): return False
        return pad or a[4] != e[6] or (a[2] - e[0]) % a[4] == 0

    def wait(q, tok):
        s, n = tok
        if known[q].get(s, 0) >= n: return
        Q[q].wait_ge(T.sem[s], n)
        k = known[q]; k[s] = n
        for s2, n2 in clock.get(tok, {}).items():
            if k.get(s2, 0) < n2: k[s2] = n2

    def emit(q, fn, R, W, sem=None, after=(), last=True, grp_tok=None):
        dma = sem is not None
        need = {}
        acc_all = [(r, False) for r in R] + [(w, True) for w in W]
        for acc, wr in acc_all:
            ps = psum(acc[1])
            for e in hist.get(acc[1], []):
                w2, q2, tok, d2 = e[2:6]
                if ps:
                    if q2 == q and (q == "pe" or not ((wr or w2) and meet(acc, e, False))): continue
                else:
                    if not (wr or w2) or not meet(acc, e, wr and w2 and dma != d2): continue
                    if dma and d2 and tok[0] == sem: continue
                if need.get(tok[0], 0) < tok[1]: need[tok[0]] = tok[1]
        for tok in after:
            if need.get(tok[0], 0) < tok[1]: need[tok[0]] = tok[1]
        for s, n in sorted(need.items(), key=lambda e: -len(clock.get(e, {}))): wait(q, (s, n))
        ins = fn()
        s = sem if dma else q
        inc = 16 if dma else 1
        if last:
            ins.then_inc(T.sem[s], inc); cnt[s] = cnt.get(s, 0) + inc
            tok = grp_tok or (s, cnt[s])
        else:
            tok = (s, cnt.get(s, 0) + 1)
        c = clock.setdefault(tok, {})
        for s2, n2 in known[q].items():
            if c.get(s2, 0) < n2: c[s2] = n2
        for acc, wr in acc_all:
            h = hist.setdefault(acc[1], [])
            if wr and acc[4] == 1:
                h[:] = [e for e in h if not (acc[2] <= e[0] and e[1] <= acc[3] and acc[5] <= e[7] and e[8] <= acc[6]
                                             and (e[4][0] == tok[0] or known[q].get(e[4][0], 0) >= e[4][1]))]
            h.append((acc[2], acc[3], wr, q, tok, dma, acc[4], acc[5], acc[6]))
        return tok

    def sc(x): return x[0] if isinstance(x, tuple) else x

    def mm(out, lhsT, rhs, start, stop, last=None, after=()):
        return emit("pe", lambda: g.tensor.matmul(out[0], lhsT[0], rhs[0], start, stop), [lhsT, rhs], [out],
                    last=stop if last is None else last, after=after)
    def group(out, terms, start=True, stop=True, last=None):
        for n, (l, r) in enumerate(terms):
            e = n == len(terms) - 1
            mm(out, l, r, start and n == 0, stop and e, last=(e and (stop if last is None else last)))
    def ts(out, in0, s1, s2, op0, op1=None):
        R = [in0] + [s for s in (s1, s2) if isinstance(s, tuple)]
        if op1 is None:
            return emit("dve", lambda: g.vector.tensor_scalar(out[0], in0[0], sc(s1), None, op0), R, [out])
        return emit("dve", lambda: g.vector.tensor_scalar(out[0], in0[0], sc(s1), sc(s2), op0, op1), R, [out])
    def tt(out, a, b, op):
        return emit("dve", lambda: g.vector.tensor_tensor(out[0], a[0], b[0], op), [a, b], [out])
    def cp(out, a):
        return emit("dve", lambda: g.vector.tensor_copy(out[0], a[0]), [a], [out])
    def ms(out, v):
        return emit("dve", lambda: g.vector.memset(out[0], v), [], [out])
    def scan(out, d0, d1, init, op0, op1):
        return emit("dve", lambda: g.vector.tensor_tensor_scan(out[0], d0[0], d1[0], init, op0, op1), [d0, d1], [out])
    def act(out, a, f, bias=0.0, scale=1.0):
        return emit("act", lambda: g.scalar.activation(out[0], a[0], f, bias=bias, scale=scale), [a], [out])
    def gat(q, name, c0, win, off, a, b, op=None):
        out, o = V(name, c0 + a, c0 + b), V(off, a // 16, b // 16)
        if op is not None:
            z = V("zr", a, b)
            return emit(q, lambda: g.vector.tensor_tensor(out[0], win[0].indirect(o[0]), z[0], op), [win, o, z], [out])
        if q == "dve":
            return emit(q, lambda: g.vector.tensor_copy(out[0], win[0].indirect(o[0])), [win, o], [out])
        return emit(q, lambda: g.scalar.activation(out[0], win[0].indirect(o[0]), F.Copy), [win, o], [out])
    def iota(out, pat, base, cm):
        if SB[out[1]][1] == i32:
            return emit("pool", lambda: g.iota(out[0], pat, base, cm), [], [out])
        return emit("pool", lambda: g.iota(out[0], pat, base, cm, allow_small_or_imprecise_dtypes=True), [], [out])
    def dma(q, sem, out, in_, R, W, grp_tok=None):
        return emit(q, lambda: Q[q].dma_start(out, in_), R, W, sem=sem, grp_tok=grp_tok)
    def I(s): return V(iname(s))
    def P(b, c0=0, c1=128, st=1, p0=0, p1=128): return V("P%d" % b, c0, c1, st, p0, p1)

    nxt, nx2, prv = cores[(rank + 1) % N], cores[(rank + 2) % N], cores[(rank - 1) % N]
    m2 = topo.mask(core, nx2)
    direct = topo.may_write(core, nxt)
    hop = nxt if direct else relay_of(core, nxt, topo)
    m1 = topo.mask(core, hop)
    n_hi = nbits(topo.mask(prv, core)) if topo.may_write(prv, core) \
        else nbits(topo.mask(relay_of(prv, core, topo), core))
    n_lo = nbits(topo.mask(cores[(rank - 2) % N], core))
    sent = [0]

    def send(dst, name, buf, sem, mask):
        rid, pid = topo.addr(dst, core)
        for e in hist.get(buf[1], []):
            if e[2] and e[0] < buf[3] and buf[2] < e[1]: wait("pool", e[4])
        g.remote_dma(T[name][:], buf[0], T.sem[sem], T.sem.sent, pid, rid, mask)
        sent[0] += nbits(mask)

    def table(t):
        tm = ("tm%d" % t, 16 * 10); tsp = ("ts%d" % t, 16 * 3)
        R = [V("src")]; W = [V("tab", 0, S0)]
        for c in range(4):
            dma("sp", tm[0], T.tab[c::16, (3 - c) * PITCH:(19 - c) * PITCH], T.src[:, 0:PITCH], R, W, tm)
        for c in range(1, 4):
            for j in range(c):
                s = 19 - c + j
                dma("sp", tm[0], T.tab[c::16, s * PITCH:(s + 1) * PITCH], T.src[j::16, 1:PITCH + 1], R, W, tm)
        for c in range(1, 4):
            dma("sp", tsp[0], T.tab[c::16, S0:TABW], T.src[:, 128 * c:128 * c + 128], R, [V("tab", S0, TABW)], tsp)

    def halves(nb):
        a = 16 * nb; m = a + (128 - nb) // 4 * 32
        return [(a, m), (m, 2048)]

    def sums(bank, buf, c0, sel, p1=128, stop=False, p0=0, js=range(16)):
        for j in js:
            mm(P(bank, j, 128, 16, p0, p1), V(buf, c0 + 16 * p0 + j, c0 + 16 * p1, 16), sel, False, stop and j == 15)

    def zdist(c0, off, ab, pre=None, mid=None):
        hs = halves(ND); vs = [(0, 16 * ND - YB), (16 * ND - YB, 16 * ND)]
        for a, b in vs: gat("dve", "yy", c0, V("X"), off, a, b, A.subtract)
        for a, b in hs: gat("act", "yy", c0, V("X"), off, a, b)
        for n, (a, b) in enumerate(hs):
            if pre: pre(n)
            group(P(n, 0, b - a), [(V("zT"), V("nE", a - 16 * ND, b - 16 * ND)), (V("Ib"), V("yy", c0 + a, c0 + b))])
            act(V(ab, a, b), P(n, 0, b - a), F.Abs)
        for n, (a, b) in enumerate(vs):
            ts(V(ab, a, b), V("yy", c0 + a, c0 + b), 0.0, 2.0, A.max, A.mult)
            if n == 0 and mid: mid()

    def xdiffs(t, win, op, mid=None, mid2=None):
        hs = halves(NX)
        gat("dve", "xb", 16, win, "ox", 16 * (NX - 16), 16 * NX, op)
        gat("dve", "xb", 16, win, "ox", 0, 16 * (NX - 16), op)
        mm(P(4), V("onf", 0, 128, 1, 0, 8), V("thE", 128 * t, 128 * t + 128, 1, 0, 8), True, False)
        for n, (a, b) in enumerate(hs):
            gat("act", "xb", 16, win, "ox", a, b)
            if n == 0 and mid: mid()
            group(P(n, 0, b - a), [(V("Ib"), V("xb", 16 + a, 16 + b)), (V("nIb"), V("xb", 15 + a, 15 + b))])
            if n == 0 and mid2: mid2(0)
        scan(V("mx", 0, 16 * NX), V("xb", 15, 15 + 16 * NX), V("xb", 16, 16 + 16 * NX), 1024.0, A.min, A.max)
        for n, (a, b) in enumerate(hs):
            act(V("mx", a, b), P(n, 0, b - a), F.Abs, scale=0.5)
            if mid2: mid2(n + 1)
        for j in range(16):
            mm(P(7, j, 128, 16, 0, NX), V("xb", 16 + j, 16 + 16 * NX, 16), V("g9", 1, 9), True, True, last=j == 15)
        act(V("Ssh", 1, 129, 1, 0, NX), P(7, 0, 128, 1, 0, NX), F.Copy)
        if t > 0:
            blockscan(16 * NX, 2048)
            scan(V("ysc", 1, 16 * NX, 2), V("m8", 0, 8 * NX), V("mx", 1, 16 * NX, 2), 0.0, A.min, A.max)
        tt(V("Tt", 0, 128, 1, 0, NX), P(7, 0, 128, 1, 0, NX), V("Ssh", 0, 128, 1, 0, NX), A.add)
        mm(P(4, 0, 128, 16, 0, NX), V("xb", 31, 16 + 16 * NX, 16), V("g9", 0, 8), False, False)
        mm(P(4, 0, 128, 16, 0, NX), V("xb", 15, 15 + 16 * NX, 16), V("ngrp"), False, False)

    def xsums(): sums(4, "mx", 0, V("grp2"), 128, True)

    def blockscan(a, b):
        scan(V("ysc", a, b), V("m16", 0, b - a), V("xb", 16 + a, 16 + b), 0.0, A.min, A.max)

    def spread(a, b):
        scan(V("zr", a, b), V("m16", 0, b - a), V("zsp", a, b), 0.0, A.min, A.max)

    dma("sp", "dl0", T.li[:], T.l0[:], [], [V("li")])
    dma("act", "dth", T.thi[0:8, 0:3], T.th[:], [], [V("thi")])
    dma("sp", "dx0", T.X[:, 0:2048], T.x0[:, 0:2048], [], [V("X", 0, 2048)])
    dma("act", "dx1", T.X[:, 2048:4096], T.x0[:, 2048:4096], [], [V("X", 2048, 4096)])
    dma("sp", "dz", T.za[:], T.z0[:], [], [V("za")])
    iota(V("vb"), [[1, 128]], 0, -1)
    iota(V("gi"), [[-16, 8]], 0, 1)
    iota(V("stg"), [[-1, 8], [0, 16]], 0, 1)
    iota(V("st2"), [[0, 8], [1, 16]], 0, 16)
    iota(V("st3"), [[0, 8], [-384, 16]], 8576, 0)
    iota(V("jF"), [[0, 8], [1, 16]], 1, 0)
    iota(V("jB"), [[0, 8], [-1, 16]], 16, 0)
    ms(V("tab", 0, 1024), 0.0)
    for a in range(F0, F1, 1024): act(V("tab", a, min(a + 1024, F1)), V("tab", 0, min(1024, F1 - a)), F.Copy)
    iota(V("tab", F2, TABW), [[0, TABW - F2]], 0, 0)
    iota(V("c32"), [[512, 8]], 0, 32)
    ms(V("tab", 1024, F0), 0.0)
    dma("sp", "dfl", T.tab[:, F1:F2], T.tab[:, 0:F2 - F1], [V("tab", 0, F2 - F1), V("X")], [V("tab", F1, F2)])
    iota(V("zsp", 0, 16 * ND), [[0, 16 * ND]], 0, 0)
    emit("pool", lambda: g.affine_select(T.nE[:], T.zsp[:, 0:2048 - 16 * ND], [[1, 128 - ND], [0, 16]], A.not_equal, -1.0, ND, -1),
         [V("zsp", 0, 2048 - 16 * ND)], [V("nE")])
    iota(V("m16"), [[0, MW // 16], [256, 16]], 0, 0)
    ts(V("Ib"), V("vb"), 0.0, None, A.is_equal)
    ts(V("nIb"), V("vb"), 0.0, -1.0, A.is_equal, A.mult)
    ts(V("gj"), V("gi"), 4, None, A.arith_shift_right)
    ms(V("ZB"), 0.0); ms(V("ZF"), 0.0); ms(V("ZH"), 0.0); ms(V("xb", 0, 16), -1024.0); ms(V("onf"), 1.0)
    ts(V("grp"), V("gj"), 0.0, None, A.is_equal)
    ts(V("ngrp"), V("gj"), 0.0, -1.0, A.is_equal, A.mult)
    ts(V("grp2"), V("gj"), 0.0, 2.0, A.is_equal, A.mult)
    ts(V("Egf"), V("stg"), 0.0, None, A.is_equal)
    cp(V("ox"), V("li"))
    cp(V("thf", 0, 3, 1, 0, 8), V("thi", 0, 3, 1, 0, 8))
    def threshold(t):
        ts(V("thE", 128 * t, 128 * t + 128, 1, 0, 8), V("Egf", 0, 128, 1, 0, 8), V("thf", t, t + 1, 1, 0, 8), -1.0, A.mult, A.mult)
    threshold(0)
    ms(V("src", 512, 528), 0.0); ms(V("OB"), 1.0)
    for p in range(4):
        ts(V("dgi", 128 * p, 128 * p + 128), V("li"), 3 * (3 - p), 7, A.logical_shift_right, A.bitwise_and)

    def digits(n):
        if n == 1:
            cp(V("src", 0, 512), V("dgi")); table(0)
        if n == 2:
            act(V("onF", 0, 128, 16), V("onf", 0, 8), F.Copy, scale=BIG)
            act(V("onB", 15, 128, 16), V("onf", 0, 8), F.Copy, scale=BIG)
            act(V("c16"), V("onf"), F.Copy, scale=16.0); act(V("onh"), V("onf"), F.Copy)
            act(I(2048), V("Ib"), F.Copy, scale=2048.0)
    xdiffs(0, V("X"), None, None, digits)
    act(V("Eg"), V("Egf"), F.Copy)
    xsums()
    group(P(3), [(V("Eg", 0, 128, 1, 0, 8), V("Eg", 0, 128, 1, 0, 8))], last=False)
    group(P(3, 128, 256), [(V("za"), V("Ib"))])
    act(I(1), V("Ib"), F.Copy)
    act(V("dlt"), V("st3"), F.Copy, scale=1.0 / 1024)
    act(V("dlt", 0, 128, 16), V("onf", 0, 8), F.Copy, scale=385.0 / 1024)
    act(V("kc"), V("st2"), F.Copy)
    for s in SCALES[2:11]: act(I(s), V("Ib"), F.Copy, scale=float(s))
    act(V("GG"), P(3), F.Copy); act(V("nGG"), P(3), F.Copy, scale=-1.0); act(V("GGb"), P(3), F.Copy)

    def fill(n):
        if n == 0:
            cp(V("s33", 0, 1), V("Ib", 112, 113)); cp(V("s33", 1, 9), V("Ib", 0, 128, 16))
            cp(V("s26", 0, 8), V("Ib", 1, 128, 16))
        if n == 1:
            cp(V("s26", 8, 16), V("Ib", 2, 128, 16)); cp(V("s26", 16, 18), V("Ib", 99, 128, 16)); cp(V("s26", 18, 26), V("Ib", 3, 128, 16))
        if n == 2:
            ms(V("zr", 16 * ND, 16 * max(NX, NL, ND + 1)), 0.0)
        if n == 5:
            ts(V("gj"), V("c32"), 9, None, A.arith_shift_right)
            ts(V("thf", 1, 3, 1, 0, 8), V("thf", 1, 3, 1, 0, 8), M32, None, A.add)
        if n == 6:
            threshold(1); cp(V("sel"), V("grp"))
            ts(V("uf", 0, 1), V("gj", 0, 1), 512.0, None, A.mult)
            ms(V("c24"), M32 / 2048)
            ts(V("c32h"), V("c32"), V("uf", 0, 1), None, A.subtract)
            ts(V("uf", 1, 2), V("c32h", 0, 1), 1.0 / 32, V("st2", 0, 1), A.mult, A.add)
        if n == 7:
            ts(V("qm"), V("st2"), V("uf", 1, 2), None, A.is_equal)
        if n == 8:
            threshold(2); ts(I(-8208), V("vb"), 0.0, -8208.0, A.is_equal, A.mult)

    Y, Z = V("ysc", 15, 2048, 16), V("zsp", 0, 2048, 16)
    ii, jj, kc, took = V("ii"), V("jj"), V("kc"), V("took")
    cs = [V("cc", 128 * n, 128 * n + 128) for n in range(3)]
    cv = [V("cv", 128 * n, 128 * n + 128) for n in range(3)]
    for t in range(RO):
        d0n, dgn, hin, lwn = "d0_%d" % t, "dg_%d" % t, "hi_%d" % t, "lw_%d" % t
        d0, d1, d2, d3 = V(d0n, 16, 144), V(dgn, 0, 128), V(dgn, 128, 256), V(dgn, 288, 416)

        if t > 0:
            group(P(3), [(V("Ib"), Y), (V("nIb"), Z)], last=False)
            group(P(3, 256, 384), [(Y, V("GGb"))], last=False)
            group(P(3, 128, 256), [(Y, V("Ib")), (Z, V("nIb"))], last=False)
            group(P(3, 384, 512), [(V("Ib"), Y), (V("Ib"), Z)])
            act(Z, P(3), F.Abs)
            act(V("hA"), P(3, 256, 384), F.Identity, bias=M32 - 15.5)
        act(V("zT"), P(3, 128, 256), F.Abs)
        tt(V("nb", 0, 128), P(4), V("Tt"), A.is_le)
        scan(V("il"), V("onF"), V("nb", 0, 128), 0.0, A.add, A.mult)
        scan(V("wl", 0, 128, -1), V("onB", 0, 128, -1), V("nb", 0, 128, -1), 0.0, A.add, A.mult)
        group(P(7, 0, 128, 1, 0, 8), [(V("il", 15, 128, 16), V("Ib"))])
        group(P(0, 0, 128, 1, 0, 8), [(V("wl", 0, 128, 16), V("Ib"))])
        scan(V("jl", 0, 128, -1), V("nb", 1, 129, -1), V("onB", 0, 128, -1), 0.0, A.mult, A.add)
        group(P(5), [(V("Ib"), V("jF"))], stop=False); group(P(6), [(V("Ib"), V("jB"))], stop=False)
        mm(P(1), I(2048), V("onh"), True, False)
        scan(V("Ibuf", 1, 129, 1, 0, 8), V("c16", 0, 128, 1, 0, 8), P(7, 0, 128, 1, 0, 8), 0.0, A.add, A.min)
        scan(V("Wbuf", 0, 128, -1, 0, 8), V("c16", 0, 128, 1, 0, 8), P(0, 0, 128, -1, 0, 8), 0.0, A.add, A.min)
        group(P(5), [(V("Ibuf", 0, 128, 1, 0, 8), V("Eg", 0, 128, 1, 0, 8))], start=False)
        group(P(4, 128, 256), [(I(1), V("dlt"))], stop=False)
        group(P(6), [(V("Wbuf", 1, 129, 1, 0, 8), V("Eg", 0, 128, 1, 0, 8))], start=False)
        group(P(2), [(I(1), kc)], stop=False)
        group(P(7), [(kc, I(1))], stop=False)
        if t > 0: group(P(3, 256, 384), [(I(2048), V("c24")), (Y, V("GGb")), (I(-1), V("hA"))])
        tt(ii, P(5), V("il"), A.min)
        tt(jj, P(6), V("jl"), A.min)
        mm(P(0), I(3), ii, True, False); mm(P(5), I(1), ii, True, False); mm(P(1), I(-1), ii, False, False)
        mm(P(0), I(-1), jj, False, True); mm(P(5), I(-1), jj, False, True)
        group(P(6), [(I(1), ii), (I(-3), jj)])
        mm(P(1), I(-1), jj, False, True)
        if t > 0: spread(0, 8 * ND)
        else: fill(0)
        group(P(2), [(I(3), ii)], start=False, stop=False)
        group(P(7), [(ii, I(3))], start=False, stop=False)
        group(P(4, 128, 256), [(I(-16), ii), (I(-16), jj)], start=False)
        for n, b in enumerate((0, 5, 6)): ts(cs[n], P(b), 0.0, None, A.is_ge)
        act(V("dv"), P(4, 128, 256), F.Relu, bias=32.0, scale=2.0)
        group(P(0), [(I(1), jj), (I(-3), ii)], stop=False)
        group(P(5), [(I(1), kc), (I(2), ii), (I(-1), jj)], stop=False)
        group(P(0), [(I(2048), c) for c in cs], start=False, stop=False)
        for n in range(3):
            tt(cv[n], P(1), cs[n], A.mult)
            mm(P(2), I(1), cv[n], False, n == 2)
            mm(P(7), cv[n], I(1), False, False)
        group(P(0), [(I(-1), c) for c in cv], start=False)
        group(P(5), [(I(1), c) for c in cv], start=False)
        for c in range(3):
            act(V("mk", MK[c], MK[c] + 128), P(0), F.Relu, bias=-8.0 * (c + 1), scale=8.0)
        if t > 0:
            tt(V("CS"), P(3, 256, 384), V("qm"), A.mult)
            ts(V("zh"), P(3, 384, 512), 0.5, -0.25, A.mult, A.add)
        else: fill(1)
        ts(V("h0"), P(2), 1.0 / 16, HC, A.mult, A.add)
        group(P(7), [(V("h0"), I(-16)), (V("h0"), I(R512))], start=False)
        if t > 0: group(P(3, 0, 8), [(V("CS"), V("sel")), (I(1), V("c32h"))])
        group(P(4), [(kc, I(1)), (ii, I(2)), (jj, I(-1))] + [(c, I(1)) for c in cv] + [(V("dv"), I(1))], stop=False)
        if t > 0: spread(8 * ND, 16 * ND)
        else: fill(2)
        ts(V("o0"), P(7), 512.0, 8191 * MAG + 3 * PITCH, A.mult, A.add)
        ts(V("h1"), P(5), 1.0 / 16, HC + 128, A.mult, A.add)
        group(P(4), [(V("h1"), I(-16)), (V("h1"), I(R512))], start=False)
        W0, W1 = V("tab", 0, S0), V("tab")
        gat("act", "G0", 0, W0, "o0", 0, G0S)
        gat("dve", "G0", 0, W0, "o0", G0S, G0S + G0A)
        if t > 0: cp(V("oc"), P(3, 0, 8))
        ts(V("o1"), P(4), 512.0, 8191 * MAG + 3 * PITCH + 512 * 2048, A.mult, A.add)
        gat("dve", "G0", 0, W0, "o0", G0S + G0A, 2048)
        act(V("mk", 256, 288), V("mk", 384, 416), F.Copy)
        for j in range(16):
            mm(P(7, j, 144, 16), V("G0", j, 2048, 16), V("s33", 0, 9), True, True, last=j == 15)
        gat("dve", "G1", 0, W1, "o1", 2048 - G1A, 2048)
        cp(V(d0n), P(7, 0, 144))
        send(hop, hin if direct else "rl_%d" % t, V(d0n, 0, 128), ("ah%d" if direct else "ar%d") % t, m1)
        for j in range(16):
            mm(P(0, j, 416, 16), V("G0", j, 2048, 16), V("s26", 0, 26), True, True, last=j == 15)
        mm(P(1, 0, 416), I(-1), V("mk"), True, False)
        if t == 0: act(Z, V("za"), F.Copy)
        gat("dve", "G1", 0, W1, "o1", G1S, 2048 - G1A)
        gat("act", "G1", 0, W1, "o1", 0, G1S)
        for j in range(16):
            mm(P(1, j, 416, 16), V("G1", j, 2048, 16), V("s26", 0, 26), False, j == 15)
        tt(V("ta"), P(0, 0, 416), V("mk"), A.min)
        if t == 0: spread(0, 8 * ND); spread(8 * ND, 16 * ND)
        if t == 0: fill(5)
        else:
            emit("dve", lambda: g.vector.tensor_copy(T.X[:].indirect(T.oc[:]), T.zh[:]), [V("oc"), V("zh")], [V("X")])
        tt(V(dgn, 256, 416), P(1, 256, 416), V("ta", 256, 416), A.max)
        send(nx2, lwn, V(dgn, 256, 384), "al%d" % t, m2)
        if t == 0: iota(V("m8", 0, 8 * NX), [[0, NX], [256, 8]], 0, 0)
        tt(V(dgn, 0, 256), P(1, 0, 256), V("ta", 0, 256), A.max)
        mid = [(d1, I(64)), (d2, I(8))]
        group(P(6), [(d0, I(512)), (d3, I(1))] + mid)
        group(P(5), mid, stop=False)
        group(P(7), [(kc, I(1))], stop=False)
        group(P(4), [(I(1), V("zer"))], stop=False)
        cp(V("oP"), P(6))
        if t < RO - 1:
            for n, d in enumerate((d0, d1, d2, d3)): mm(P(2, 128 * n, 128 * n + 128), d, I(1), n == 0, False)
        else:
            group(P(2), mid + [(d0, I(512)), (d3, I(1))], stop=False)

        def name_m():
            mm(P(5), V(lwn), I(1), False, False, after=[("al%d" % t, n_lo)])
            mm(P(5), V(hin), I(512), False, True, after=[("ah%d" % t, n_hi)])
            cp(V("oM"), P(5))
            sums(4, "yy", 0, V("grp"), ND)
        zdist(0, "oP", "aby", None, name_m)
        zdist(2048, "oM", "ab2", lambda n: sums(4, "aby", 0, V("ngrp"), js=range(RY) if n == 0 else range(RY, 16)))
        sums(4, "yy", 2048, V("ngrp"), ND)
        sums(4, "ab2", 0, V("grp"), 128, True)
        if t == 0: fill(6); fill(7)
        mm(P(3), I(1), V(hin), True, False); mm(P(3), I(-1), d0, False, False)
        mm(P(3, 128, 256), I(1), V(lwn), False, False); mm(P(3, 128, 256), I(-1), d3, False, False)
        ts(took, P(4), 0.0, None, A.is_lt)
        group(P(7), [(took, I(2048))], start=False)
        mm(P(3), I(64), took, False, False); mm(P(3, 128, 256), I(64), took, False, True)
        if t == 0: fill(8)
        cp(V("ox"), P(7))
        r0, r3 = V("rl", 0, 128), V("rl", 128, 256)
        if t < RO - 1:
            act(V("rl"), P(3, 0, 256), F.Relu, bias=-48.0)
            group(P(5), [(took, V("onh"))])

            def names():
                group(P(2, 0, 128), [(r0, I(1)), (took, I(-16))], start=False, stop=False)
                group(P(2, 384, 512), [(r3, I(1)), (took, I(-16))], start=False)
                act(V("CS"), P(5), F.Copy)

            def count(n):
                if n == 0:
                    group(P(6), [(V("CS"), V("GG"))])
                    group(P(4), [(V("CS"), V("nGG"))], start=False, stop=False)
                if n == 1: act(V("hA"), P(6), F.Identity, bias=M32 - 15.5)
            xdiffs(t + 1, V("yy"), A.add, names, count)
            act(V("src", 0, 512), P(2, 0, 512), F.Copy); table(t + 1)
            group(P(4), [(I(1), V("hA"))], start=False, stop=False)
            xsums()
        else:
            def xq(a, b, e, q):
                gat(e, "xb", 16, V("yy"), "ox", a, b, A.add if e == "dve" else None)
                dma("sp", "oxy%d" % q, T.xy[:, a:b], T.xb[:, 16 + a:16 + b], [V("xb", 16 + a, 16 + b)], [])
            h = halves(NL); m = 32 * (NL // 6)
            xq(0, m, "dve", 0); xq(h[0][0], h[0][1], "act", 1)
            xq(h[1][0], h[1][1], "act", 3); xq(m, 16 * NL, "dve", 2)
            act(V("rl"), P(3, 0, 256), F.Relu, bias=-48.0)
            group(P(2), [(r0, I(512)), (r3, I(1)), (took, I(-8208))], start=False)
            act(V("lo"), P(2), F.Copy)
            dma("act", "oly", T.ly[:], T.lo[:], [V("lo")], [])
            blockscan(0, m); blockscan(16 * NL, 2048); blockscan(m, 16 * NL)
            group(P(3), [(V("Ib"), Y), (V("nIb"), Z)])
            act(V("zo"), P(3), F.Abs)
            dma("act", "ozy", T.zy[:], T.zo[:], [V("zo")], [])
    for s in ["pe", "dve", "act", "pool"] + DSEMS:
        if cnt.get(s, 0): g.wait_ge(T.sem[s], cnt[s])
    g.wait_ge(T.sem.sent, sent[0])
